import numpy as np, ml_dtypes
CORES = [8,136,40,168]
N = 4
BF = ml_dtypes.bfloat16
S, R, B, CAP = 512, 128, 4, 288
L, IT, I = 4, 4, 16
D, TOP, F = 2, 2, 1
def where_to(rep):
    i = np.arange(N * S); first = np.maximum.accumulate(np.where(rep == 0, i, 0)); rec = np.add.accumulate((rep == 0).astype(np.int64)) - 1
    kth = np.add.accumulate((rep == 1).astype(np.int64)); head = np.maximum.accumulate(np.where(rep < 2, i, 0))
    return rec, kth - kth[first], i - head
def count(rec):
    return np.bincount(np.arange(N * S) // S * N + rec // B % N, minlength=N * N)
def parts(rng, lens, total):
    diff = int(total - np.sum(lens)); room = I - lens if diff > 0 else lens - 1
    k = np.bincount(rng.permutation(np.repeat(np.arange(len(lens)), room))[:abs(diff)], minlength=len(lens))
    return lens + (k if diff > 0 else -k)
def rich(rng, n, total):
    return parts(rng, np.where(rng.random(n) * ((I - 1) * n) < 2 * (total - n), rng.integers(1, I + 1, n), 1), total)
def levels(rng, lens):
    if count(np.repeat(np.arange(len(lens)), lens)).max() > CAP:
        lens = np.diff(np.arange(N * R + 1) * (N * S) // (N * R))
    rep = np.full(N * S, TOP, np.int32); rep[np.add.accumulate(lens) - lens] = 0
    if L > 1:
        u = rng.random(N * S).tolist(); i = 0
        for n in lens.tolist():
            k = c = 1
            for j in range(1, n):
                if c == IT or (k < L and n - j <= (L - k) * IT and u[i + j] < 0.35):
                    rep[i + j] = 1; k += 1; c = 1
                else: c += 1
            i += n
    return rep
def values(rng):
    return rng.integers(0, 1 << 20, (N, 8, S)).astype(np.int32)
def make(rng, cols, p):
    rl = np.ascontiguousarray(np.stack([levels(rng, c) for c in cols]).reshape(8, N, S).transpose(1, 0, 2))
    dl = np.where(rng.random((N, 8, S)) < p, D, rng.integers(0, D, (N, 8, S))).astype(np.int32)
    return {"rl": rl, "dl": dl, "val": values(rng)}
def setup_inputs(rng):
    cols = [rich(rng, int(rng.integers(N * R * 3 // 4, N * R + 1)), N * S) for g in range(8)]
    return make(rng, cols, rng.integers(4, 16, (N, 8, 1)) * 0.0625)
def setup_inputs_full(rng):
    cols = []; mix = rng.permutation(8).tolist(); odd = mix[:4]; home = mix[4]; m = R // N
    for g in range(8):
        if g in odd: cols.append(rich(rng, N * R, N * S)); continue
        c = []
        for q in range(N):
            d = q if g == home else (q + 1 + g % (N - 1)) % N; own = np.arange(R) // B % N == d; v = np.ones(R, np.int64)
            v[own] = parts(rng, v[own], CAP); v[~own] = parts(rng, v[~own], S - CAP); c.append(v)
        cols.append(np.concatenate(c))
    return make(rng, cols, rng.choice(np.array([0.5, 1.0]), (N, 8, 1)))
def setup_inputs_edges(rng):
    cols = []
    for g in range(8):
        a = rng.integers(0, I + 1, N - 1); c = []; at = 0
        if g < 4: a[:] = (0, I, 1, I - 1)[g]
        for q in range(1, N + 1):
            end = q * S - int(a[q - 1]) if q < N else N * S; seg = end - at
            c.append(rich(rng, max(-(-seg // I), seg * R * int(rng.integers(12, 17)) // (16 * S)), seg))
            if q < N: c.append(np.array([I])); at = end + I
        cols.append(np.concatenate(c))
    return make(rng, cols, rng.integers(0, 3, (N, 8, 1)) * 0.5)
def setup_inputs_few(rng):
    cols = []
    for g in range(8):
        h = int(rng.integers(1, I + 1)) if g else I; k = (N * S - h) // I; t = N * S - h - k * I
        cols.append(np.array([h] + [I] * k + ([t] if t else [])))
    p = rng.integers(8, 17, (N, 8, 1)) * 0.0625; p[:, rng.integers(0, 8)] = 0
    return make(rng, cols, p)
def setup_inputs_spread(rng):
    cols = [rich(rng, int(rng.integers(N * S // I, N * R + 1)), N * S) for g in range(8)]
    d = make(rng, cols, rng.integers(1, 16, (N, 8, 1)) * 0.0625)
    v = d["val"] >> rng.integers(0, 21, (N, 8, S)); d["val"] = np.where(rng.random((N, 8, S)) < 0.0625, (1 << 20) - 1, v).astype(np.int32)
    return d
def check_inputs(d):
    rl, dl, val = d["rl"], d["dl"], d["val"]; bad = []
    if not (((rl >= 0) & (rl <= TOP)).all() and ((dl >= 0) & (dl <= D)).all()): bad.append("levels")
    if not (rl[0, :, 0] == 0).all(): bad.append("first")
    if not (((val >= 0) & (val < 1 << 20)).all()): bad.append("values")
    if bad: return bad
    for g in range(8):
        rec, lst, item = where_to(rl[:, g].reshape(-1))
        if rec[-1] >= N * R: bad.append("records")
        if lst.max() >= L or item.max() >= IT: bad.append("items")
        if count(rec).max() > CAP: bad.append("pairs")
    return sorted(set(bad))
def reference(rl, dl, val):
    y = np.full((N, 8, F, R * I), -2, np.float32); x = val.reshape(N, 8, F, S); q = np.arange(N * S) // S
    for g in range(8):
        rec, lst, item = where_to(rl[:, g].reshape(-1)); lev = dl[:, g].reshape(-1)
        has = (dl[:, g] == D).astype(np.int64); v = (np.add.accumulate(has, axis=1) - has).reshape(-1)
        e = np.where((lev == D)[:, None], x[q, g, :, v].astype(np.float32), (lev - D)[:, None])
        y[rec // B % N, g, :, (rec // (B * N) * B + rec % B) * I + lst * IT + item] = e
    return {"y": y.reshape(N, 8 * F, R * I).astype(np.float32)}

@@ -1,0 +1,215 @@
+from concourse.bass import DstId, RemoteDMATransfer
+from concourse.mybir import dt, AluOpType as A, AxisListType, ActivationFunctionType as F
+
+WINW = 512 + 16 * 512
+SCRATCH = {
+    "rlt": ("sbuf", [128, 32], "int32"), "dlt": ("sbuf", [128, 32], "int32"),
+    "rlw": ("sbuf", [128, 32], "int32"), "dlw": ("sbuf", [128, 32], "int32"),
+    "rlr": ("sbuf", [128, 512], "int32"),
+    "vw": ("sbuf", [128, 1048], "int32"),
+    "f0": ("sbuf", [128, 48], "bfloat16"), "sm": ("sbuf", [128, 48], "bfloat16"),
+    "f2": ("sbuf", [128, 32], "bfloat16"), "s2": ("sbuf", [128, 32], "bfloat16"),
+    "cap": ("sbuf", [128, 32], "float32"), "ovf": ("sbuf", [128, 32], "float32"),
+    "offv": ("sbuf", [128, 32], "uint16"), "offs": ("sbuf", [128, 32], "uint16"),
+    "rb": ("sbuf", [128, 544], "bfloat16"), "one4": ("sbuf", [128, 512], "bfloat16"),
+    "d0": ("sbuf", [128, 512], "bfloat16"), "rst": ("sbuf", [128, 512], "bfloat16"),
+    "ls": ("sbuf", [128, 512], "bfloat16"), "pl": ("sbuf", [128, 512], "bfloat16"),
+    "one4h": ("sbuf", [128, 32], "bfloat16"), "d0h": ("sbuf", [128, 32], "bfloat16"),
+    "lsh": ("sbuf", [128, 32], "bfloat16"), "plh": ("sbuf", [128, 32], "bfloat16"),
+    "mask": ("sbuf", [128, 512], "bfloat16"), "maskh": ("sbuf", [128, 16], "bfloat16"),
+    "mm": ("sbuf", [128, 512], "float32"), "mmh": ("sbuf", [128, 16], "float32"),
+    "vv": ("sbuf", [128, 512], "float32"),
+    "win": ("sbuf", [128, WINW], "float32"),
+    "msg0": ("sbuf", [128, 24], "bfloat16"), "msg1": ("sbuf", [128, 24], "bfloat16"),
+    "land1": ("sbuf", [128, 128], "float32"), "land2": ("sbuf", [128, 128], "float32"), "land3": ("sbuf", [128, 128], "float32"),
+    "acc1": ("sbuf", [128, 128], "float32"), "acc2": ("sbuf", [128, 128], "float32"),
+    "ta": ("sbuf", [128, 4, 32], "float32"), "tl": ("sbuf", [128, 4, 32], "float32"),
+    "fin": ("sbuf", [128, 2, 4, 16], "float32"),
+    "ones": ("sbuf", [128, 128], "bfloat16"), "sga": ("sbuf", [128, 128], "bfloat16"), "sg": ("sbuf", [128, 128], "bfloat16"),
+    "lt": ("sbuf", [128, 128], "bfloat16"), "d1": ("sbuf", [128, 128], "bfloat16"), "d2": ("sbuf", [128, 128], "bfloat16"),
+    "b8": ("sbuf", [128, 128], "bfloat16"),
+    "a1": ("sbuf", [128, 128], "bfloat16"), "a2": ("sbuf", [128, 128], "bfloat16"), "a3": ("sbuf", [128, 128], "bfloat16"),
+    "a4": ("sbuf", [128, 128], "bfloat16"), "lv": ("sbuf", [128, 128], "bfloat16"), "d1s": ("sbuf", [128, 128], "bfloat16"),
+    "d2s": ("sbuf", [128, 128], "bfloat16"),
+    "pi": ("sbuf", [128, 1], "int32"), "pa": ("sbuf", [128, 1], "int32"),
+    "wcol": ("sbuf", [128, 1], "float32"), "pcol": ("sbuf", [128, 1], "float32"), "kcol": ("sbuf", [128, 1], "float32"),
+    "hi": ("sbuf", [128, 32], "int32"), "uu": ("sbuf", [128, 32], "float32"), "zz": ("sbuf", [128, 32], "float32"),
+    "ps1": ("psum", [128, 512], "float32"), "ps2": ("psum", [128, 512], "float32"), "psv": ("psum", [128, 512], "float32"),
+    "psb": ("psum", [128, 512], "float32"), "psw": ("psum", [128, 512], "float32"), "psr": ("psum", [128, 512], "float32"),
+    "psh": ("psum", [128, 512], "float32"),
+}
+SEMAPHORES = ["s%d" % i for i in range(110)] + ["m0", "m1", "m2", "h0", "h1", "h2", "h3", "loc1", "loc2"]
+BIG = float(1 << 22)
+
+
+def rank_program(g, core, T, topo):
+    r = T.rank_of(core)
+    if r is None:
+        return
+    N = len(T.cores)
+    V, S, P, Y = g.vector, g.scalar, g.tensor, g.sync
+    queues = {"g": g, "v": V, "s": S, "p": P, "y": Y}
+    seen = {q: [] for q in queues}
+    used = []
+
+    def after(q, deps):
+        for d in deps:
+            if d is not None and d not in seen[q]:
+                queues[q].wait_ge(T.sem[d[0]], d[1])
+                seen[q].append(d)
+
+    def new():
+        used.append("s%d" % len(used))
+        return used[-1]
+
+    def do(q, call, deps=()):
+        after(q, deps)
+        n = new()
+        call(queues[q]).then_inc(T.sem[n], 1)
+        return (n, 1)
+
+    def load(parts):
+        n = new()
+        for q, out, in_ in parts:
+            queues[q].dma_start(out, in_).then_inc(T.sem[n], 16)
+        return (n, 16 * len(parts))
+
+    ins = {"rl": T.rl, "dl": T.dl}
+    l_rlt = load([("y", T.rlt[:, 0:16], T.rl[0::2, :]), ("s", T.rlt[:, 16:32], T.rl[1::2, :])])
+    l_rlr = load([("y", T.rlr[0:8, :], T.rl[:, :])])
+    l_dlt = load([("s", T.dlt[:, 0:16], T.dl[0::2, :]), ("y", T.dlt[:, 16:32], T.dl[1::2, :])])
+    l_val = load([("sy"[w % 2], T.vw[w::16, 0:512], T.val[:, :]) for w in range(16)])
+
+    ones = do("v", lambda e: e.memset(T.ones[:, :], 1.0))
+    sga = do("g", lambda e: e.affine_select(T.sga[:, :], T.ones[:, :], [[-16, 8], [0, 16]], A.is_ge, 0.0, 0, 1), [ones])
+    sg = do("g", lambda e: e.affine_select(T.sg[:, :], T.sga[:, :], [[16, 8], [0, 16]], A.is_ge, 0.0, 15, -1), [sga])
+    lt = do("g", lambda e: e.affine_select(T.lt[:, :], T.sg[:, :], [[-1, 128]], A.is_ge, 0.0, -1, 1), [sg])
+    pi = do("g", lambda e: e.iota(T.pi[:, :], [[0, 1]], 0, 1))
+    d1 = do("g", lambda e: e.affine_select(T.d1[:, :], T.lt[:, :], [[-1, 128]], A.is_equal, 0.0, -1, 1), [lt])
+    d2 = do("g", lambda e: e.affine_select(T.d2[:, :], T.sg[:, :], [[1, 128]], A.is_equal, 0.0, -15, -1), [sg])
+    b8 = do("g", lambda e: e.affine_select(T.b8[0:8, :], T.ones[0:8, :], [[1, 8], [0, 16]], A.is_equal, 0.0, 0, -1))
+    f1 = do("v", lambda e: e.memset(T.f0[:, 32:48], 1.0))
+    tz = do("v", lambda e: e.memset(T.sm[:, 32:48], 0.0))
+    wf = do("v", lambda e: e.memset(T.win[:, 0:512], -2.0))
+    vn = do("v", lambda e: e.memset(T.vw[:, 512:1040], -1))
+    vz = do("v", lambda e: e.memset(T.vw[:, 1040:1048], -2))
+    pa = do("v", lambda e: e.tensor_scalar(T.pa[:, :], T.pi[:, :], 15, None, A.bitwise_and), [pi])
+    wcol = do("v", lambda e: e.tensor_scalar(T.wcol[:, :], T.pa[:, :], 1.0, None, A.mult), [pa])
+    pcol = do("v", lambda e: e.tensor_scalar(T.pcol[:, :], T.pa[:, :], 512.0, 480.0, A.mult, A.add), [pa])
+    kcol = do("v", lambda e: e.tensor_scalar(T.kcol[:, :], T.pa[:, :], -512.0, None, A.mult), [pa])
+
+    def scaled(out, in_, c, dep):
+        return do("s", lambda e: e.activation(out[:, :], in_[:, :], F.Copy, scale=c), [dep])
+    a1 = scaled(T.a1, T.sg, 0.0625, sg)
+    a3 = scaled(T.a3, T.sg, 32.0, sg)
+    a2 = scaled(T.a2, T.lt, -0.0625, lt)
+    a4 = scaled(T.a4, T.lt, -32.0, lt)
+    lv = scaled(T.lv, T.lt, -1.0, lt)
+    d2s = scaled(T.d2s, T.d2, -8192.0, d2)
+
+    rlw = do("v", lambda e: e.transpose(T.rlw[:, :], T.rlt[:, :]), [l_rlt])
+    f0 = do("v", lambda e: e.tensor_scalar(T.f0[:, 0:32], T.rlw[:, :], 0.0, None, A.is_equal), [rlw])
+    s0 = do("v", lambda e: e.tensor_tensor_scan(T.sm[:, 0:32], T.f0[:, 0:32], T.f0[:, 0:32], 0.0, A.add, A.max), [f0])
+    later = [d for d in range(r + 1, N)]
+    if later:
+        tail = do("v", lambda e: e.tensor_scalar(T.sm[0:8, 32:48], T.rlr[0:8, 496:512], 16.0, None, A.mult), [tz, l_rlr])
+        after("g", [s0, tail])
+        ids, dsts = [], []
+        for d in reversed(later):
+            rid, pnc = topo.addr(T.cores[d], core)
+            ids.append(DstId(rid=rid, pnc=pnc))
+            dsts.append(T.rb[:, 15:32] if d == r + 1 else T["msg%d" % r][:, 0:17])
+        msk = topo.mask(core, T.cores[later[0]])
+        g.remote_dma_fused([RemoteDMATransfer(dst_ids=ids, dma_engine_mask=msk, remote_sem=T.sem["m%d" % r],
+                                              srcs=[T.sm[:, 31:48]], dsts=dsts)], local_sem=T.sem["loc1"])
+        n_loc1 = len(topo.engines(core, T.cores[later[0]]))
+
+    rb = do("v", lambda e: e.tensor_scalar(T.rb[0:8, 32:544], T.rlr[0:8, :], 16.0, None, A.mult), [l_rlr])
+    d0 = do("s", lambda e: e.activation(T.d0[0:8, :], T.rb[0:8, 32:544], F.Copy, bias=-31.0), [rb])
+    rst = do("s", lambda e: e.activation(T.rst[0:8, :], T.rb[0:8, 32:544], F.Copy, bias=-2.0, scale=float(1 << 17)), [rb])
+    dlw = do("v", lambda e: e.transpose(T.dlw[:, :], T.dlt[:, :]), [l_dlt])
+    one4 = do("v", lambda e: e.tensor_scalar(T.one4[0:8, :], T.rb[0:8, 32:544], 16.0, 4.0, A.is_equal, A.mult), [rb])
+    f2 = do("v", lambda e: e.tensor_scalar(T.f2[:, :], T.dlw[:, :], 2.0, None, A.is_equal), [dlw])
+    cap = do("v", lambda e: e.tensor_scalar(T.cap[:, :], T.dlw[:, :], -520.0, 1041.0, A.mult, A.add))
+    s2 = do("v", lambda e: e.tensor_tensor_scan(T.s2[:, :], T.f2[:, :], T.f2[:, :], 0.0, A.add, A.max), [f2])
+    ls = do("v", lambda e: e.tensor_tensor_scan(T.ls[0:8, :], T.one4[0:8, :], T.rb[0:8, 32:544], 0.0, A.add, A.min), [one4])
+    pl = do("v", lambda e: e.tensor_tensor_scan(T.pl[0:8, :], T.d0[0:8, :], T.ls[0:8, :], 0.0, A.add, A.max), [d0, ls])
+    d1s = do("v", lambda e: e.tensor_scalar(T.d1s[:, :], T.d1[:, :], T.kcol[:, :], None, A.mult), [kcol, d1])
+
+    v1 = do("p", lambda e: e.matmul(T.psv[:, 0:32], T.lv[:, :], T.f2[:, :], True, False), [lv, f2])
+    v2 = do("p", lambda e: e.matmul(T.psv[:, 0:32], T.sg[:, :], T.s2[:, :], False, True), [sg, s2])
+    psw = do("p", lambda e: e.matmul(T.psw[:, :], T.b8[0:8, :], T.pl[0:8, :], True, True), [b8, pl])
+    psr = do("p", lambda e: e.matmul(T.psr[:, :], T.b8[0:8, :], T.rst[0:8, :], True, True), [rst])
+    r1 = do("p", lambda e: e.matmul(T.ps1[:, 0:32], T.a1[:, :], T.sm[:, 0:32], True, False), [a1, s0])
+    r2 = do("p", lambda e: e.matmul(T.ps1[:, 0:32], T.a2[:, :], T.f0[:, 0:32], False, True), [a2, f0])
+    q1 = do("p", lambda e: e.matmul(T.ps2[:, 0:32], T.a3[:, :], T.sm[:, 0:32], True, False), [a3])
+    q2 = do("p", lambda e: e.matmul(T.ps2[:, 0:32], T.a4[:, :], T.f0[:, 0:32], False, False), [a4])
+    q3 = do("p", lambda e: e.matmul(T.ps2[:, 0:32], T.d1s[:, :], T.f0[:, 0:32], False, False), [d1s])
+    q4 = do("p", lambda e: e.matmul(T.ps2[:, 0:32], T.d2s[:, :], T.f0[:, 1:33], False, True), [d2s, f1])
+
+    ovf = do("v", lambda e: e.tensor_tensor(T.ovf[:, :], T.cap[:, :], T.psv[:, 0:32], A.max), [cap, v1, v2])
+    offv = do("v", lambda e: e.tensor_scalar(T.offv[:, :], T.ovf[:, :], -1.0, None, A.add), [ovf])
+    mask = do("v", lambda e: e.tensor_scalar(T.mask[:, :], T.psw[:, :], T.wcol[:, :], -BIG, A.not_equal, A.mult), [psw, wcol])
+    mm = do("v", lambda e: e.tensor_tensor(T.mm[:, :], T.vw[:, 0:1048].indirect(T.offv[:, 0:32]), T.mask[:, :], A.add),
+            [l_val, vn, vz, offv, mask])
+    vv = do("v", lambda e: e.tensor_tensor_scan(T.vv[:, :], T.psr[:, :], T.mm[:, :], -2.0, A.min, A.max), [psr, mm])
+
+    if r:
+        eng = len(topo.engines(T.cores[0], core))
+        heads = [("m%d" % p, eng) for p in range(r)]
+        mine = heads[r - 1]
+        cnt = [T["msg%d" % p][:, 0:1] for p in range(r - 1)] + [T.rb[:, 15:16]]
+        one4h = do("v", lambda e: e.tensor_scalar(T.one4h[0:8, :], T.rb[0:8, 16:48], 16.0, 4.0, A.is_equal, A.mult), [mine])
+        d0h = do("v", lambda e: e.tensor_scalar(T.d0h[0:8, :], T.rb[0:8, 16:48], -31.0, None, A.add))
+        lsh = do("v", lambda e: e.tensor_tensor_scan(T.lsh[0:8, :], T.one4h[0:8, :], T.rb[0:8, 16:48], 0.0, A.add, A.min), [one4h])
+        plh = do("v", lambda e: e.tensor_tensor_scan(T.plh[0:8, :], T.d0h[0:8, :], T.lsh[0:8, :], 0.0, A.add, A.max), [d0h, lsh])
+        base = []
+        for col, mat in ((0, T.a1), (1, T.a3)):
+            for p in range(r):
+                base.append(do("p", lambda e: e.matmul(T.psb[:, col:col + 1], mat[:, :], cnt[p], p == 0, p == r - 1), [heads[p]]))
+        psh = do("p", lambda e: e.matmul(T.psh[:, 0:16], T.b8[0:8, :], T.plh[0:8, 16:32], True, True), [plh])
+        hi = do("v", lambda e: e.tensor_scalar(T.hi[:, :], T.ps1[:, 0:32], T.psb[:, 0:1], -17.0 / 32, A.add, A.add), [r1, r2] + base)
+        uu = do("v", lambda e: e.tensor_scalar(T.uu[:, :], T.hi[:, :], -511.0, T.pcol[:, :], A.mult, A.add), [hi, pcol])
+        maskh = do("v", lambda e: e.tensor_scalar(T.maskh[:, :], T.psh[:, 0:16], T.wcol[:, :], -BIG, A.not_equal, A.mult), [psh])
+        zz = do("v", lambda e: e.tensor_tensor(T.zz[:, :], T.uu[:, :], T.ps2[:, 0:32], A.add), [uu, q1, q2, q3, q4])
+        mmh = do("v", lambda e: e.tensor_tensor(T.mmh[:, :], T.vw[:, 0:1048].indirect(T.offv[:, 0:1]), T.maskh[:, :], A.add), [maskh])
+        offs = do("v", lambda e: e.tensor_scalar(T.offs[:, :], T.zz[:, :], T.psb[:, 1:2], None, A.add), [zz])
+        vvh = do("v", lambda e: e.tensor_tensor_scan(T.vv[:, 0:16], T.psr[:, 0:16], T.mmh[:, :], -2.0, A.min, A.max), [mmh, vv])
+    else:
+        hi = do("v", lambda e: e.tensor_scalar(T.hi[:, :], T.ps1[:, 0:32], -17.0 / 32, None, A.add), [r1, r2])
+        uu = do("v", lambda e: e.tensor_scalar(T.uu[:, :], T.hi[:, :], -511.0, T.pcol[:, :], A.mult, A.add), [hi, pcol])
+        zz = do("v", lambda e: e.tensor_tensor(T.zz[:, :], T.uu[:, :], T.ps2[:, 0:32], A.add), [uu, q1, q2, q3, q4])
+        offs = do("v", lambda e: e.tensor_copy(T.offs[:, :], T.zz[:, :]), [zz])
+        vvh = vv
+
+    sc = do("v", lambda e: e.tensor_copy(T.win[:, 0:WINW].indirect(T.offs[:, 0:32]), T.vv[:, :]), [offs, vvh, wf])
+
+    after("g", [sc])
+    n_loc2 = 0
+    for k in range(1, N):
+        d = (r + k) % N
+        rid, pnc = topo.addr(T.cores[d], core)
+        g.remote_dma(T["land%d" % k][:, :], T.win[:, 128 * d:128 * d + 128], T.sem["h%d" % k], T.sem["loc2"],
+                     pnc, rid, topo.mask(core, T.cores[d]))
+        n_loc2 += len(topo.engines(core, T.cores[d]))
+    arr = [None] + [("h%d" % k, len(topo.engines(T.cores[(r - k) % N], core))) for k in range(1, N)]
+    c1 = do("v", lambda e: e.tensor_tensor(T.acc1[:, :], T.win[:, 128 * r:128 * r + 128], T.land1[:, :], A.max), [sc, arr[1]])
+    c2 = do("v", lambda e: e.tensor_tensor(T.acc2[:, :], T.acc1[:, :], T.land2[:, :], A.max), [c1, arr[2]])
+    ta = [do("v", lambda e: e.transpose(T.ta[:, b, :], T.acc2[:, 32 * b:32 * b + 32]), [c2]) for b in range(4)]
+    tl = [do("v", lambda e: e.transpose(T.tl[:, b, :], T.land3[:, 32 * b:32 * b + 32]), [arr[3]]) for b in range(4)]
+    fin = [do("v", lambda e: e.tensor_tensor(T.fin[:, h, :, :], T.ta[:, :, 16 * h:16 * h + 16], T.tl[:, :, 16 * h:16 * h + 16], A.max),
+              ta + tl) for h in range(2)]
+    for h, q in enumerate("ys"):
+        after(q, [fin[h]])
+        n = new()
+        queues[q].dma_start(T.y[h::2, :], T.fin[:, h, :, :]).then_inc(T.sem[n], 16)
+        queues[q].wait_ge(T.sem[n], 16)
+        seen[q].append((n, 16))
+
+    if later:
+        g.wait_ge(T.sem["loc1"], n_loc1)
+    g.wait_ge(T.sem["loc2"], n_loc2)
+    waited = [d[0] for q in seen for d in seen[q]]
+    for n in used:
+        if n not in waited:
+            g.wait_ge(T.sem[n], 1)

@@ -1,44 +1,36 @@
 from concourse.bass import DstId, RemoteDMATransfer
-from concourse.mybir import dt, AluOpType as A, AxisListType, ActivationFunctionType as F
+from concourse.mybir import AluOpType as A, ActivationFunctionType as F
 
 WINW = 512 + 16 * 512
+VWW = 536
+I32, F32, B16, U16 = "int32", "float32", "bfloat16", "uint16"
+
+
+def sb(width, dtype):
+    return ("sbuf", [128] + (width if isinstance(width, list) else [width]), dtype)
+
+
 SCRATCH = {
-    "rlt": ("sbuf", [128, 32], "int32"), "dlt": ("sbuf", [128, 32], "int32"),
-    "rlw": ("sbuf", [128, 32], "int32"), "dlw": ("sbuf", [128, 32], "int32"),
-    "rlr": ("sbuf", [128, 512], "int32"),
-    "vw": ("sbuf", [128, 1048], "int32"),
-    "f0": ("sbuf", [128, 48], "bfloat16"), "sm": ("sbuf", [128, 48], "bfloat16"),
-    "f2": ("sbuf", [128, 32], "bfloat16"), "s2": ("sbuf", [128, 32], "bfloat16"),
-    "cap": ("sbuf", [128, 32], "float32"), "ovf": ("sbuf", [128, 32], "float32"),
-    "offv": ("sbuf", [128, 32], "uint16"), "offs": ("sbuf", [128, 32], "uint16"),
-    "rb": ("sbuf", [128, 544], "bfloat16"), "one4": ("sbuf", [128, 512], "bfloat16"),
-    "d0": ("sbuf", [128, 512], "bfloat16"), "rst": ("sbuf", [128, 512], "bfloat16"),
-    "ls": ("sbuf", [128, 512], "bfloat16"), "pl": ("sbuf", [128, 512], "bfloat16"),
-    "one4h": ("sbuf", [128, 32], "bfloat16"), "d0h": ("sbuf", [128, 32], "bfloat16"),
-    "lsh": ("sbuf", [128, 32], "bfloat16"), "plh": ("sbuf", [128, 32], "bfloat16"),
-    "mask": ("sbuf", [128, 512], "bfloat16"), "maskh": ("sbuf", [128, 16], "bfloat16"),
-    "mm": ("sbuf", [128, 512], "float32"), "mmh": ("sbuf", [128, 16], "float32"),
-    "vv": ("sbuf", [128, 512], "float32"),
-    "win": ("sbuf", [128, WINW], "float32"),
-    "msg0": ("sbuf", [128, 24], "bfloat16"), "msg1": ("sbuf", [128, 24], "bfloat16"),
-    "land1": ("sbuf", [128, 128], "float32"), "land2": ("sbuf", [128, 128], "float32"), "land3": ("sbuf", [128, 128], "float32"),
-    "acc1": ("sbuf", [128, 128], "float32"), "acc2": ("sbuf", [128, 128], "float32"),
-    "ta": ("sbuf", [128, 4, 32], "float32"), "tl": ("sbuf", [128, 4, 32], "float32"),
-    "fin": ("sbuf", [128, 2, 4, 16], "float32"),
-    "ones": ("sbuf", [128, 128], "bfloat16"), "sga": ("sbuf", [128, 128], "bfloat16"), "sg": ("sbuf", [128, 128], "bfloat16"),
-    "lt": ("sbuf", [128, 128], "bfloat16"), "d1": ("sbuf", [128, 128], "bfloat16"), "d2": ("sbuf", [128, 128], "bfloat16"),
-    "b8": ("sbuf", [128, 128], "bfloat16"),
-    "a1": ("sbuf", [128, 128], "bfloat16"), "a2": ("sbuf", [128, 128], "bfloat16"), "a3": ("sbuf", [128, 128], "bfloat16"),
-    "a4": ("sbuf", [128, 128], "bfloat16"), "lv": ("sbuf", [128, 128], "bfloat16"), "d1s": ("sbuf", [128, 128], "bfloat16"),
-    "d2s": ("sbuf", [128, 128], "bfloat16"),
-    "pi": ("sbuf", [128, 1], "int32"), "pa": ("sbuf", [128, 1], "int32"),
-    "wcol": ("sbuf", [128, 1], "float32"), "pcol": ("sbuf", [128, 1], "float32"), "kcol": ("sbuf", [128, 1], "float32"),
-    "hi": ("sbuf", [128, 32], "int32"), "uu": ("sbuf", [128, 32], "float32"), "zz": ("sbuf", [128, 32], "float32"),
-    "ps1": ("psum", [128, 512], "float32"), "ps2": ("psum", [128, 512], "float32"), "psv": ("psum", [128, 512], "float32"),
-    "psb": ("psum", [128, 512], "float32"), "psw": ("psum", [128, 512], "float32"), "psr": ("psum", [128, 512], "float32"),
-    "psh": ("psum", [128, 512], "float32"),
+    "rlt": sb(32, I32), "dlt": sb(32, I32), "rlw": sb(32, I32), "dlw": sb(32, I32), "rlc": sb(144, I32), "tli": sb(16, I32),
+    "vw": sb(VWW, I32), "f0": sb(48, B16), "sm": sb(48, B16), "f2": sb(32, B16), "s2": sb(32, B16),
+    "cap": sb(32, F32), "ovf": sb(32, F32), "offv": sb(32, U16), "offs": sb(32, U16),
+    "rb": sb(144, B16), "one4": sb(144, B16), "d0": sb(144, B16), "ls": sb(144, B16), "pl": sb(144, B16), "rst": sb(128, B16),
+    "rbh": sb(48, B16), "one4h": sb(32, B16), "d0h": sb(32, B16), "lsh": sb(32, B16), "plh": sb(32, B16),
+    "mask": sb(512, B16), "maskh": sb(16, B16), "mm": sb(512, F32), "mmh": sb(16, F32), "vv": sb(512, F32),
+    "win": sb(WINW, F32), "msg0": sb(24, B16), "msg1": sb(24, B16),
+    "from0": sb(128, F32), "from1": sb(128, F32), "from2": sb(128, F32), "from3": sb(128, F32),
+    "acc1": sb(128, F32), "acc2": sb(128, F32), "ta": sb([4, 32], F32), "tl": sb([4, 32], F32), "fin": sb([2, 4, 16], F32),
+    "mg": sb(128, B16), "sg": sb(128, B16), "lt": sb(128, B16), "d1": sb(128, B16), "d2": sb(128, B16),
+    "sel0": sb(128, B16), "sel1": sb(128, B16), "sel2": sb(128, B16), "sel3": sb(128, B16),
+    "a1": sb(128, B16), "a2": sb(128, B16), "a3": sb(128, B16), "a4": sb(128, B16), "lv": sb(128, B16),
+    "d1s": sb(128, B16), "d2s": sb(128, B16),
+    "pi": sb(1, I32), "pa": sb(1, I32), "kg": sb(1, I32), "pif": sb(1, F32), "kgf": sb(1, F32),
+    "wcol": sb(1, F32), "mb": sb(1, F32), "pcol": sb(1, F32), "kcol": sb(1, F32),
+    "hi": sb(32, I32), "uu": sb(32, F32), "zz": sb(32, F32),
 }
-SEMAPHORES = ["s%d" % i for i in range(110)] + ["m0", "m1", "m2", "h0", "h1", "h2", "h3", "loc1", "loc2"]
+for _b in ("ps1", "ps2", "psv", "psb", "psh", "psw0", "psw1", "psr"):
+    SCRATCH[_b] = ("psum", [128, 512], "float32")
+SEMAPHORES = ["s%d" % i for i in range(120)] + ["m0", "m1", "m2", "h0", "h1", "h2", "h3", "loc1", "loc2"]
 BIG = float(1 << 22)
 
 
@@ -47,14 +39,13 @@ def rank_program(g, core, T, topo):
     if r is None:
         return
     N = len(T.cores)
-    V, S, P, Y = g.vector, g.scalar, g.tensor, g.sync
-    queues = {"g": g, "v": V, "s": S, "p": P, "y": Y}
+    queues = {"g": g, "v": g.vector, "s": g.scalar, "p": g.tensor, "y": g.sync}
     seen = {q: [] for q in queues}
     used = []
 
     def after(q, deps):
         for d in deps:
-            if d is not None and d not in seen[q]:
+            if d not in seen[q]:
                 queues[q].wait_ge(T.sem[d[0]], d[1])
                 seen[q].append(d)
 
@@ -74,137 +65,161 @@ def rank_program(g, core, T, topo):
             queues[q].dma_start(out, in_).then_inc(T.sem[n], 16)
         return (n, 16 * len(parts))
 
-    ins = {"rl": T.rl, "dl": T.dl}
+    def ts(out, in0, s1, op0, s2=None, op1=None, deps=()):
+        if op1 is None:
+            return do("v", lambda e: e.tensor_scalar(out, in0, s1, None, op0), deps)
+        return do("v", lambda e: e.tensor_scalar(out, in0, s1, s2, op0, op1), deps)
+
+    def scan(out, x0, x1, initial, op0, op1, deps=()):
+        return do("v", lambda e: e.tensor_tensor_scan(out, x0, x1, initial, op0, op1), deps)
+
+    def mat(out, lhs, rhs, start, stop, deps=()):
+        return do("p", lambda e: e.matmul(out, lhs, rhs, start, stop), deps)
+
     l_rlt = load([("y", T.rlt[:, 0:16], T.rl[0::2, :]), ("s", T.rlt[:, 16:32], T.rl[1::2, :])])
-    l_rlr = load([("y", T.rlr[0:8, :], T.rl[:, :])])
-    l_dlt = load([("s", T.dlt[:, 0:16], T.dl[0::2, :]), ("y", T.dlt[:, 16:32], T.dl[1::2, :])])
+    l_tli = load([("s", T.tli[0:8, :], T.rl[:, 496:512])]) if r < N - 1 else None
+    l_rlc = load([("y", T.rlc[0:8, 16:144], T.rl[:, 0:128])] +
+                 [("sy"[a % 2], T.rlc[8 * a:8 * a + 8, :], T.rl[:, 128 * a - 16:128 * a + 128]) for a in (3, 2, 1)])
+    l_dlt = load([("y", T.dlt[:, 0:16], T.dl[0::2, :]), ("s", T.dlt[:, 16:32], T.dl[1::2, :])])
     l_val = load([("sy"[w % 2], T.vw[w::16, 0:512], T.val[:, :]) for w in range(16)])
 
-    ones = do("v", lambda e: e.memset(T.ones[:, :], 1.0))
-    sga = do("g", lambda e: e.affine_select(T.sga[:, :], T.ones[:, :], [[-16, 8], [0, 16]], A.is_ge, 0.0, 0, 1), [ones])
-    sg = do("g", lambda e: e.affine_select(T.sg[:, :], T.sga[:, :], [[16, 8], [0, 16]], A.is_ge, 0.0, 15, -1), [sga])
-    lt = do("g", lambda e: e.affine_select(T.lt[:, :], T.sg[:, :], [[-1, 128]], A.is_ge, 0.0, -1, 1), [sg])
     pi = do("g", lambda e: e.iota(T.pi[:, :], [[0, 1]], 0, 1))
-    d1 = do("g", lambda e: e.affine_select(T.d1[:, :], T.lt[:, :], [[-1, 128]], A.is_equal, 0.0, -1, 1), [lt])
-    d2 = do("g", lambda e: e.affine_select(T.d2[:, :], T.sg[:, :], [[1, 128]], A.is_equal, 0.0, -15, -1), [sg])
-    b8 = do("g", lambda e: e.affine_select(T.b8[0:8, :], T.ones[0:8, :], [[1, 8], [0, 16]], A.is_equal, 0.0, 0, -1))
-    f1 = do("v", lambda e: e.memset(T.f0[:, 32:48], 1.0))
+    mg = do("g", lambda e: e.iota(T.mg[:, :], [[1, 8], [0, 16]], 0, 0, allow_small_or_imprecise_dtypes=True))
+    hz = do("v", lambda e: e.memset(T.rlc[0:8, 0:16], 0))
     tz = do("v", lambda e: e.memset(T.sm[:, 32:48], 0.0))
-    wf = do("v", lambda e: e.memset(T.win[:, 0:512], -2.0))
-    vn = do("v", lambda e: e.memset(T.vw[:, 512:1040], -1))
-    vz = do("v", lambda e: e.memset(T.vw[:, 1040:1048], -2))
-    pa = do("v", lambda e: e.tensor_scalar(T.pa[:, :], T.pi[:, :], 15, None, A.bitwise_and), [pi])
-    wcol = do("v", lambda e: e.tensor_scalar(T.wcol[:, :], T.pa[:, :], 1.0, None, A.mult), [pa])
-    pcol = do("v", lambda e: e.tensor_scalar(T.pcol[:, :], T.pa[:, :], 512.0, 480.0, A.mult, A.add), [pa])
-    kcol = do("v", lambda e: e.tensor_scalar(T.kcol[:, :], T.pa[:, :], -512.0, None, A.mult), [pa])
+    kg = ts(T.kg[:, :], T.pi[:, :], 4, A.arith_shift_right, deps=[pi])
+    pa = ts(T.pa[:, :], T.pi[:, :], 15, A.bitwise_and)
+    kgf = do("v", lambda e: e.tensor_copy(T.kgf[:, :], T.kg[:, :]), [kg])
+    sg = ts(T.sg[:, :], T.mg[:, :], T.kgf[:, :], A.is_equal, deps=[mg, kgf])
+    lt = do("g", lambda e: e.affine_select(T.lt[:, :], T.sg[:, :], [[-1, 128]], A.is_ge, 0.0, -1, 1), [sg])
+    d2 = do("g", lambda e: e.affine_select(T.d2[:, :], T.sg[:, :], [[1, 128]], A.is_equal, 0.0, -15, -1), [sg])
+    d1 = do("g", lambda e: e.affine_select(T.d1[:, :], T.lt[:, :], [[-1, 128]], A.is_equal, 0.0, -1, 1), [lt])
+    pif = do("v", lambda e: e.tensor_copy(T.pif[:, :], T.pi[:, :]))
+    wcol = ts(T.wcol[:, :], T.pa[:, :], 1.0, A.mult, deps=[pa])
+    mb = ts(T.mb[:, :], T.pa[:, :], -2048.0, A.mult)
+    pcol = ts(T.pcol[:, :], T.pa[:, :], 512.0, A.mult, 480.0, A.add)
+    kcol = ts(T.kcol[:, :], T.pa[:, :], -512.0, A.mult)
+    sel = [ts(T["sel%d" % a][0:32, :], T.mg[0:32, :], 8.0 * a, A.add, T.pif[0:32, :], A.is_equal, [pif]) for a in range(4)]
+    f1 = do("v", lambda e: e.memset(T.f0[:, 32:48], 1.0))
+    vn = do("v", lambda e: e.memset(T.vw[:, 512:528], -1))
+    vz = do("v", lambda e: e.memset(T.vw[:, 528:536], -2))
 
     def scaled(out, in_, c, dep):
         return do("s", lambda e: e.activation(out[:, :], in_[:, :], F.Copy, scale=c), [dep])
     a1 = scaled(T.a1, T.sg, 0.0625, sg)
     a3 = scaled(T.a3, T.sg, 32.0, sg)
+    lv = scaled(T.lv, T.lt, -1.0, lt)
     a2 = scaled(T.a2, T.lt, -0.0625, lt)
     a4 = scaled(T.a4, T.lt, -32.0, lt)
-    lv = scaled(T.lv, T.lt, -1.0, lt)
     d2s = scaled(T.d2s, T.d2, -8192.0, d2)
 
     rlw = do("v", lambda e: e.transpose(T.rlw[:, :], T.rlt[:, :]), [l_rlt])
-    f0 = do("v", lambda e: e.tensor_scalar(T.f0[:, 0:32], T.rlw[:, :], 0.0, None, A.is_equal), [rlw])
-    s0 = do("v", lambda e: e.tensor_tensor_scan(T.sm[:, 0:32], T.f0[:, 0:32], T.f0[:, 0:32], 0.0, A.add, A.max), [f0])
+    if r < N - 1:
+        tail = ts(T.sm[0:8, 32:48], T.tli[0:8, :], 16.0, A.mult, deps=[tz, l_tli])
+    f0 = ts(T.f0[:, 0:32], T.rlw[:, :], 0.0, A.is_equal, deps=[rlw])
+    s0 = scan(T.sm[:, 0:32], T.f0[:, 0:32], T.f0[:, 0:32], 0.0, A.add, A.max, [f0])
     later = [d for d in range(r + 1, N)]
     if later:
-        tail = do("v", lambda e: e.tensor_scalar(T.sm[0:8, 32:48], T.rlr[0:8, 496:512], 16.0, None, A.mult), [tz, l_rlr])
-        after("g", [s0, tail])
+        after("g", [tail, s0])
         ids, dsts = [], []
         for d in reversed(later):
             rid, pnc = topo.addr(T.cores[d], core)
             ids.append(DstId(rid=rid, pnc=pnc))
-            dsts.append(T.rb[:, 15:32] if d == r + 1 else T["msg%d" % r][:, 0:17])
-        msk = topo.mask(core, T.cores[later[0]])
-        g.remote_dma_fused([RemoteDMATransfer(dst_ids=ids, dma_engine_mask=msk, remote_sem=T.sem["m%d" % r],
-                                              srcs=[T.sm[:, 31:48]], dsts=dsts)], local_sem=T.sem["loc1"])
+            dsts.append(T.rbh[:, 15:32] if d == r + 1 else T["msg%d" % r][:, 0:17])
+        g.remote_dma_fused([RemoteDMATransfer(dst_ids=ids, dma_engine_mask=topo.mask(core, T.cores[later[0]]),
+                                              remote_sem=T.sem["m%d" % r], srcs=[T.sm[:, 31:48]], dsts=dsts)],
+                           local_sem=T.sem["loc1"])
         n_loc1 = len(topo.engines(core, T.cores[later[0]]))
 
-    rb = do("v", lambda e: e.tensor_scalar(T.rb[0:8, 32:544], T.rlr[0:8, :], 16.0, None, A.mult), [l_rlr])
-    d0 = do("s", lambda e: e.activation(T.d0[0:8, :], T.rb[0:8, 32:544], F.Copy, bias=-31.0), [rb])
-    rst = do("s", lambda e: e.activation(T.rst[0:8, :], T.rb[0:8, 32:544], F.Copy, bias=-2.0, scale=float(1 << 17)), [rb])
+    rb = ts(T.rb[0:32, :], T.rlc[0:32, :], 16.0, A.mult, deps=[hz, l_rlc])
+    d0 = do("s", lambda e: e.activation(T.d0[0:32, :], T.rb[0:32, :], F.Copy, bias=-31.0), [rb])
+    rst = do("s", lambda e: e.activation(T.rst[0:32, :], T.rb[0:32, 16:144], F.Copy, bias=-2.0, scale=float(1 << 17)))
+    one4 = ts(T.one4[0:32, :], T.rb[0:32, :], 16.0, A.is_equal, 4.0, A.mult, [rb])
     dlw = do("v", lambda e: e.transpose(T.dlw[:, :], T.dlt[:, :]), [l_dlt])
-    one4 = do("v", lambda e: e.tensor_scalar(T.one4[0:8, :], T.rb[0:8, 32:544], 16.0, 4.0, A.is_equal, A.mult), [rb])
-    f2 = do("v", lambda e: e.tensor_scalar(T.f2[:, :], T.dlw[:, :], 2.0, None, A.is_equal), [dlw])
-    cap = do("v", lambda e: e.tensor_scalar(T.cap[:, :], T.dlw[:, :], -520.0, 1041.0, A.mult, A.add))
-    s2 = do("v", lambda e: e.tensor_tensor_scan(T.s2[:, :], T.f2[:, :], T.f2[:, :], 0.0, A.add, A.max), [f2])
-    ls = do("v", lambda e: e.tensor_tensor_scan(T.ls[0:8, :], T.one4[0:8, :], T.rb[0:8, 32:544], 0.0, A.add, A.min), [one4])
-    pl = do("v", lambda e: e.tensor_tensor_scan(T.pl[0:8, :], T.d0[0:8, :], T.ls[0:8, :], 0.0, A.add, A.max), [d0, ls])
-    d1s = do("v", lambda e: e.tensor_scalar(T.d1s[:, :], T.d1[:, :], T.kcol[:, :], None, A.mult), [kcol, d1])
+    ls = scan(T.ls[0:32, :], T.one4[0:32, :], T.rb[0:32, :], 0.0, A.add, A.min, [one4])
+    f2 = ts(T.f2[:, :], T.dlw[:, :], 2.0, A.is_equal, deps=[dlw])
+    cap = ts(T.cap[:, :], T.dlw[:, :], -520.0, A.mult, 1041.0, A.add)
+    pl = scan(T.pl[0:32, :], T.d0[0:32, :], T.ls[0:32, :], 0.0, A.add, A.max, [d0, ls])
+    s2 = scan(T.s2[:, :], T.f2[:, :], T.f2[:, :], 0.0, A.add, A.max, [f2])
+    d1s = ts(T.d1s[:, :], T.d1[:, :], T.kcol[:, :], A.mult, deps=[kcol, d1])
+    wf = do("v", lambda e: e.memset(T.win[:, 0:512], -2.0))
 
-    v1 = do("p", lambda e: e.matmul(T.psv[:, 0:32], T.lv[:, :], T.f2[:, :], True, False), [lv, f2])
-    v2 = do("p", lambda e: e.matmul(T.psv[:, 0:32], T.sg[:, :], T.s2[:, :], False, True), [sg, s2])
-    psw = do("p", lambda e: e.matmul(T.psw[:, :], T.b8[0:8, :], T.pl[0:8, :], True, True), [b8, pl])
-    psr = do("p", lambda e: e.matmul(T.psr[:, :], T.b8[0:8, :], T.rst[0:8, :], True, True), [rst])
-    r1 = do("p", lambda e: e.matmul(T.ps1[:, 0:32], T.a1[:, :], T.sm[:, 0:32], True, False), [a1, s0])
-    r2 = do("p", lambda e: e.matmul(T.ps1[:, 0:32], T.a2[:, :], T.f0[:, 0:32], False, True), [a2, f0])
-    q1 = do("p", lambda e: e.matmul(T.ps2[:, 0:32], T.a3[:, :], T.sm[:, 0:32], True, False), [a3])
-    q2 = do("p", lambda e: e.matmul(T.ps2[:, 0:32], T.a4[:, :], T.f0[:, 0:32], False, False), [a4])
-    q3 = do("p", lambda e: e.matmul(T.ps2[:, 0:32], T.d1s[:, :], T.f0[:, 0:32], False, False), [d1s])
-    q4 = do("p", lambda e: e.matmul(T.ps2[:, 0:32], T.d2s[:, :], T.f0[:, 1:33], False, True), [d2s, f1])
+    psw = []
+    for a in range(4):
+        psw.append(mat(T["psw%d" % (a // 2)][:, 128 * (a % 2):128 * (a % 2) + 128], T["sel%d" % a][0:32, :], T.pl[0:32, 16:144],
+                       True, True, [sel[a], pl]))
+        if a == 1:
+            v1 = mat(T.psv[:, 0:32], T.lv[:, :], T.f2[:, :], True, False, [lv, f2])
+            v2 = mat(T.psv[:, 0:32], T.sg[:, :], T.s2[:, :], False, True, [sg, s2])
+    psr = [mat(T.psr[:, 128 * a:128 * a + 128], T["sel%d" % a][0:32, :], T.rst[0:32, :], True, True, [rst]) for a in range(4)]
+    ps1 = [mat(T.ps1[:, 0:32], T.a1[:, :], T.sm[:, 0:32], True, False, [a1, s0]),
+           mat(T.ps1[:, 0:32], T.a2[:, :], T.f0[:, 0:32], False, True, [a2, f0])]
+    ps2 = [mat(T.ps2[:, 0:32], T.a3[:, :], T.sm[:, 0:32], True, False, [a3]),
+           mat(T.ps2[:, 0:32], T.a4[:, :], T.f0[:, 0:32], False, False, [a4]),
+           mat(T.ps2[:, 0:32], T.d1s[:, :], T.f0[:, 0:32], False, False, [d1s]),
+           mat(T.ps2[:, 0:32], T.d2s[:, :], T.f0[:, 1:33], False, True, [d2s, f1])]
 
     ovf = do("v", lambda e: e.tensor_tensor(T.ovf[:, :], T.cap[:, :], T.psv[:, 0:32], A.max), [cap, v1, v2])
-    offv = do("v", lambda e: e.tensor_scalar(T.offv[:, :], T.ovf[:, :], -1.0, None, A.add), [ovf])
-    mask = do("v", lambda e: e.tensor_scalar(T.mask[:, :], T.psw[:, :], T.wcol[:, :], -BIG, A.not_equal, A.mult), [psw, wcol])
-    mm = do("v", lambda e: e.tensor_tensor(T.mm[:, :], T.vw[:, 0:1048].indirect(T.offv[:, 0:32]), T.mask[:, :], A.add),
-            [l_val, vn, vz, offv, mask])
-    vv = do("v", lambda e: e.tensor_tensor_scan(T.vv[:, :], T.psr[:, :], T.mm[:, :], -2.0, A.min, A.max), [psr, mm])
+    offv = ts(T.offv[:, :], T.ovf[:, :], -1.0, A.add, 528.0, A.min, [ovf])
+    mask = [do("s", lambda e: e.activation(T.mask[:, 256 * h:256 * h + 256], T["psw%d" % h][:, 0:256], F.Square,
+                                           bias=T.mb[:, :], scale=2048.0), [psw[2 * h], psw[2 * h + 1], mb]) for h in range(2)]
+    mm = [do("v", lambda e: e.tensor_tensor(T.mm[:, 256 * h:256 * h + 256], T.vw[:, 0:VWW].indirect(T.offv[:, 16 * h:16 * h + 16]),
+                                            T.mask[:, 256 * h:256 * h + 256], A.subtract), [l_val, vn, vz, offv, mask[h]])
+          for h in range(2)]
+    vv = scan(T.vv[:, :], T.psr[:, :], T.mm[:, :], -2.0, A.min, A.max, psr + mm)
 
     if r:
-        eng = len(topo.engines(T.cores[0], core))
-        heads = [("m%d" % p, eng) for p in range(r)]
-        mine = heads[r - 1]
-        cnt = [T["msg%d" % p][:, 0:1] for p in range(r - 1)] + [T.rb[:, 15:16]]
-        one4h = do("v", lambda e: e.tensor_scalar(T.one4h[0:8, :], T.rb[0:8, 16:48], 16.0, 4.0, A.is_equal, A.mult), [mine])
-        d0h = do("v", lambda e: e.tensor_scalar(T.d0h[0:8, :], T.rb[0:8, 16:48], -31.0, None, A.add))
-        lsh = do("v", lambda e: e.tensor_tensor_scan(T.lsh[0:8, :], T.one4h[0:8, :], T.rb[0:8, 16:48], 0.0, A.add, A.min), [one4h])
-        plh = do("v", lambda e: e.tensor_tensor_scan(T.plh[0:8, :], T.d0h[0:8, :], T.lsh[0:8, :], 0.0, A.add, A.max), [d0h, lsh])
+        own = ts(T.rbh[0:8, 32:48], T.rlc[0:8, 16:32], 16.0, A.mult)
+        heads = [("m%d" % p, len(topo.engines(T.cores[p], core))) for p in range(r)]
+        cnt = [T["msg%d" % p][:, 0:1] for p in range(r - 1)] + [T.rbh[:, 15:16]]
+        one4h = ts(T.one4h[0:8, :], T.rbh[0:8, 16:48], 16.0, A.is_equal, 4.0, A.mult, [own, heads[-1]])
+        d0h = ts(T.d0h[0:8, :], T.rbh[0:8, 16:48], -31.0, A.add)
+        lsh = scan(T.lsh[0:8, :], T.one4h[0:8, :], T.rbh[0:8, 16:48], 0.0, A.add, A.min, [one4h])
+        plh = scan(T.plh[0:8, :], T.d0h[0:8, :], T.lsh[0:8, :], 0.0, A.add, A.max, [d0h, lsh])
         base = []
-        for col, mat in ((0, T.a1), (1, T.a3)):
+        for col, m in ((0, T.a1), (1, T.a3)):
             for p in range(r):
-                base.append(do("p", lambda e: e.matmul(T.psb[:, col:col + 1], mat[:, :], cnt[p], p == 0, p == r - 1), [heads[p]]))
-        psh = do("p", lambda e: e.matmul(T.psh[:, 0:16], T.b8[0:8, :], T.plh[0:8, 16:32], True, True), [plh])
-        hi = do("v", lambda e: e.tensor_scalar(T.hi[:, :], T.ps1[:, 0:32], T.psb[:, 0:1], -17.0 / 32, A.add, A.add), [r1, r2] + base)
-        uu = do("v", lambda e: e.tensor_scalar(T.uu[:, :], T.hi[:, :], -511.0, T.pcol[:, :], A.mult, A.add), [hi, pcol])
-        maskh = do("v", lambda e: e.tensor_scalar(T.maskh[:, :], T.psh[:, 0:16], T.wcol[:, :], -BIG, A.not_equal, A.mult), [psh])
-        zz = do("v", lambda e: e.tensor_tensor(T.zz[:, :], T.uu[:, :], T.ps2[:, 0:32], A.add), [uu, q1, q2, q3, q4])
-        mmh = do("v", lambda e: e.tensor_tensor(T.mmh[:, :], T.vw[:, 0:1048].indirect(T.offv[:, 0:1]), T.maskh[:, :], A.add), [maskh])
-        offs = do("v", lambda e: e.tensor_scalar(T.offs[:, :], T.zz[:, :], T.psb[:, 1:2], None, A.add), [zz])
-        vvh = do("v", lambda e: e.tensor_tensor_scan(T.vv[:, 0:16], T.psr[:, 0:16], T.mmh[:, :], -2.0, A.min, A.max), [mmh, vv])
+                base.append(mat(T.psb[:, col:col + 1], m[:, :], cnt[p], p == 0, p == r - 1, [heads[p]]))
+        psh = mat(T.psh[:, 0:16], T.sel0[0:8, :], T.plh[0:8, 16:32], True, True, [plh])
+        hi = ts(T.hi[:, :], T.ps1[:, 0:32], T.psb[:, 0:1], A.add, -17.0 / 32, A.add, ps1 + base)
+        uu = ts(T.uu[:, :], T.hi[:, :], -511.0, A.mult, T.pcol[:, :], A.add, [hi, pcol])
+        maskh = ts(T.maskh[:, :], T.psh[:, 0:16], T.wcol[:, :], A.not_equal, BIG, A.mult, [psh, wcol])
+        zz = do("v", lambda e: e.tensor_tensor(T.zz[:, :], T.uu[:, :], T.ps2[:, 0:32], A.add), [uu] + ps2)
+        mmh = do("v", lambda e: e.tensor_tensor(T.mmh[:, :], T.vw[:, 0:VWW].indirect(T.offv[:, 0:1]), T.maskh[:, :], A.subtract),
+                 [maskh])
+        offs = ts(T.offs[:, :], T.zz[:, :], T.psb[:, 1:2], A.add, deps=[zz])
+        done = scan(T.vv[:, 0:16], T.psr[:, 0:16], T.mmh[:, :], -2.0, A.min, A.max, [mmh, vv])
     else:
-        hi = do("v", lambda e: e.tensor_scalar(T.hi[:, :], T.ps1[:, 0:32], -17.0 / 32, None, A.add), [r1, r2])
-        uu = do("v", lambda e: e.tensor_scalar(T.uu[:, :], T.hi[:, :], -511.0, T.pcol[:, :], A.mult, A.add), [hi, pcol])
-        zz = do("v", lambda e: e.tensor_tensor(T.zz[:, :], T.uu[:, :], T.ps2[:, 0:32], A.add), [uu, q1, q2, q3, q4])
+        hi = ts(T.hi[:, :], T.ps1[:, 0:32], -17.0 / 32, A.add, deps=ps1)
+        uu = ts(T.uu[:, :], T.hi[:, :], -511.0, A.mult, T.pcol[:, :], A.add, [hi, pcol])
+        zz = do("v", lambda e: e.tensor_tensor(T.zz[:, :], T.uu[:, :], T.ps2[:, 0:32], A.add), [uu] + ps2)
         offs = do("v", lambda e: e.tensor_copy(T.offs[:, :], T.zz[:, :]), [zz])
-        vvh = vv
+        done = vv
 
-    sc = do("v", lambda e: e.tensor_copy(T.win[:, 0:WINW].indirect(T.offs[:, 0:32]), T.vv[:, :]), [offs, vvh, wf])
+    sc = do("v", lambda e: e.tensor_copy(T.win[:, 0:WINW].indirect(T.offs[:, 0:32]), T.vv[:, :]), [offs, done, wf])
 
     after("g", [sc])
     n_loc2 = 0
     for k in range(1, N):
         d = (r + k) % N
         rid, pnc = topo.addr(T.cores[d], core)
-        g.remote_dma(T["land%d" % k][:, :], T.win[:, 128 * d:128 * d + 128], T.sem["h%d" % k], T.sem["loc2"],
+        g.remote_dma(T["from%d" % r][:, :], T.win[:, 128 * d:128 * d + 128], T.sem["h%d" % r], T.sem["loc2"],
                      pnc, rid, topo.mask(core, T.cores[d]))
         n_loc2 += len(topo.engines(core, T.cores[d]))
-    arr = [None] + [("h%d" % k, len(topo.engines(T.cores[(r - k) % N], core))) for k in range(1, N)]
-    c1 = do("v", lambda e: e.tensor_tensor(T.acc1[:, :], T.win[:, 128 * r:128 * r + 128], T.land1[:, :], A.max), [sc, arr[1]])
-    c2 = do("v", lambda e: e.tensor_tensor(T.acc2[:, :], T.acc1[:, :], T.land2[:, :], A.max), [c1, arr[2]])
+    src = [p for p in range(N) if p != r]
+    arr = [("h%d" % p, len(topo.engines(T.cores[p], core))) for p in src]
+    land = [T["from%d" % p] for p in src]
+    c1 = do("v", lambda e: e.tensor_tensor(T.acc1[:, :], T.win[:, 128 * r:128 * r + 128], land[0][:, :], A.max), [sc, arr[0]])
+    c2 = do("v", lambda e: e.tensor_tensor(T.acc2[:, :], T.acc1[:, :], land[1][:, :], A.max), [c1, arr[1]])
     ta = [do("v", lambda e: e.transpose(T.ta[:, b, :], T.acc2[:, 32 * b:32 * b + 32]), [c2]) for b in range(4)]
-    tl = [do("v", lambda e: e.transpose(T.tl[:, b, :], T.land3[:, 32 * b:32 * b + 32]), [arr[3]]) for b in range(4)]
+    tl = [do("v", lambda e: e.transpose(T.tl[:, b, :], land[2][:, 32 * b:32 * b + 32]), [arr[2]]) for b in range(4)]
     fin = [do("v", lambda e: e.tensor_tensor(T.fin[:, h, :, :], T.ta[:, :, 16 * h:16 * h + 16], T.tl[:, :, 16 * h:16 * h + 16], A.max),
               ta + tl) for h in range(2)]
     for h, q in enumerate("ys"):
         after(q, [fin[h]])
         n = new()
         queues[q].dma_start(T.y[h::2, :], T.fin[:, h, :, :]).then_inc(T.sem[n], 16)
-        queues[q].wait_ge(T.sem[n], 16)
-        seen[q].append((n, 16))
+        after(q, [(n, 16)])
 
     if later:
         g.wait_ge(T.sem["loc1"], n_loc1)

@@ -1,8 +1,10 @@
 from concourse.bass import DstId, RemoteDMATransfer
 from concourse.mybir import AluOpType as A, ActivationFunctionType as F
 
-WINW = 512 + 16 * 512
-VWW = 536
+H = 26
+BLK, COLS = 4 * H, 16 * H
+WINW = 17 * COLS
+VWW = 16 + 512
 I32, F32, B16, U16 = "int32", "float32", "bfloat16", "uint16"
 
 
@@ -11,27 +13,26 @@ def sb(width, dtype):
 
 
 SCRATCH = {
-    "rlt": sb(32, I32), "dlt": sb(32, I32), "rlw": sb(32, I32), "dlw": sb(32, I32), "rlc": sb(144, I32), "tli": sb(16, I32),
-    "vw": sb(VWW, I32), "f0": sb(48, B16), "sm": sb(48, B16), "f2": sb(32, B16), "s2": sb(32, B16),
-    "cap": sb(32, F32), "ovf": sb(32, F32), "offv": sb(32, U16), "offs": sb(32, U16),
-    "rb": sb(144, B16), "one4": sb(144, B16), "d0": sb(144, B16), "ls": sb(144, B16), "pl": sb(144, B16), "rst": sb(128, B16),
-    "rbh": sb(48, B16), "one4h": sb(32, B16), "d0h": sb(32, B16), "lsh": sb(32, B16), "plh": sb(32, B16),
-    "mask": sb(512, B16), "maskh": sb(16, B16), "mm": sb(512, F32), "mmh": sb(16, F32), "vv": sb(512, F32),
-    "win": sb(WINW, F32), "msg0": sb(24, B16), "msg1": sb(24, B16),
-    "from0": sb(128, F32), "from1": sb(128, F32), "from2": sb(128, F32), "from3": sb(128, F32),
-    "acc1": sb(128, F32), "acc2": sb(128, F32), "ta": sb([4, 32], F32), "tl": sb([4, 32], F32), "fin": sb([2, 4, 16], F32),
-    "mg": sb(128, B16), "sg": sb(128, B16), "lt": sb(128, B16), "d1": sb(128, B16), "d2": sb(128, B16),
+    "lt0": sb(64, I32), "lw": sb(64, I32), "rlc": sb(144, I32), "vw": sb(VWW, I32),
+    "ff": sb(65, B16), "sm": sb(65, B16), "f2": sb(32, B16), "s2": sb(32, B16),
+    "mn": sb(32, F32), "offv": sb(32, U16), "offs": sb(32, U16), "hh": sb(32, B16),
+    "ca": sb(144, B16), "cb": sb(144, B16), "cp": sb(144, B16), "rst": sb(144, B16),
+    "ha": sb(48, B16), "hb": sb(48, B16), "hp": sb(48, B16),
+    "mask": sb(512, B16), "maskh": sb(32, B16), "mm": sb(512, F32), "vv": sb(512, F32), "win": sb(WINW, F32),
+    "msg0": sb(32, B16), "msg1": sb(32, B16), "msg2": sb(32, B16),
+    "from0": sb([4, H], F32), "from1": sb([4, H], F32), "from2": sb([4, H], F32), "from3": sb([4, H], F32),
+    "acc": sb([4, 32], F32), "ta": sb([4, 32], F32), "fin": sb([2, 4, 16], F32),
+    "mg": sb(128, B16), "mi": sb(128, B16), "sg": sb(128, B16), "lt": sb(128, B16), "idn": sb(128, B16), "idh": sb(128, B16),
     "sel0": sb(128, B16), "sel1": sb(128, B16), "sel2": sb(128, B16), "sel3": sb(128, B16),
-    "a1": sb(128, B16), "a2": sb(128, B16), "a3": sb(128, B16), "a4": sb(128, B16), "lv": sb(128, B16),
+    "sgv": sb(128, B16), "lvv": sb(128, B16), "sgr": sb(128, B16), "ltr": sb(128, B16),
     "d1s": sb(128, B16), "d2s": sb(128, B16),
-    "pi": sb(1, I32), "pa": sb(1, I32), "kg": sb(1, I32), "pif": sb(1, F32), "kgf": sb(1, F32),
-    "wcol": sb(1, F32), "mb": sb(1, F32), "pcol": sb(1, F32), "kcol": sb(1, F32),
-    "hi": sb(32, I32), "uu": sb(32, F32), "zz": sb(32, F32),
+    "pi": sb(1, I32), "pa": sb(1, I32), "kg": sb(1, I32), "pif": sb(1, F32), "paf": sb(1, F32), "kgf": sb(1, F32),
+    "kmod": sb(1, F32), "pm1": sb(1, F32), "p15": sb(1, F32), "zc": sb(1, F32),
+    "ccol": sb(1, F32), "mb": sb(1, F32), "pcol": sb(1, F32), "kcol": sb(1, F32),
 }
-for _b in ("ps1", "ps2", "psv", "psb", "psh", "psw0", "psw1", "psr"):
+for _b in ("ps1", "ps2", "psv", "psh", "psw0", "psw1", "psr"):
     SCRATCH[_b] = ("psum", [128, 512], "float32")
-SEMAPHORES = ["s%d" % i for i in range(120)] + ["m0", "m1", "m2", "h0", "h1", "h2", "h3", "loc1", "loc2"]
-BIG = float(1 << 22)
+SEMAPHORES = ["s%d" % i for i in range(110)] + ["m0", "m1", "m2", "t", "h0", "h1", "h2", "h3", "loc0", "loc1", "loc2"]
 
 
 def rank_program(g, core, T, topo):
@@ -73,157 +74,171 @@ def rank_program(g, core, T, topo):
     def scan(out, x0, x1, initial, op0, op1, deps=()):
         return do("v", lambda e: e.tensor_tensor_scan(out, x0, x1, initial, op0, op1), deps)
 
+    def tt(out, in0, in1, op, deps=()):
+        return do("v", lambda e: e.tensor_tensor(out, in0, in1, op), deps)
+
     def mat(out, lhs, rhs, start, stop, deps=()):
         return do("p", lambda e: e.matmul(out, lhs, rhs, start, stop), deps)
 
-    l_rlt = load([("y", T.rlt[:, 0:16], T.rl[0::2, :]), ("s", T.rlt[:, 16:32], T.rl[1::2, :])])
-    l_tli = load([("s", T.tli[0:8, :], T.rl[:, 496:512])]) if r < N - 1 else None
-    l_rlc = load([("y", T.rlc[0:8, 16:144], T.rl[:, 0:128])] +
-                 [("sy"[a % 2], T.rlc[8 * a:8 * a + 8, :], T.rl[:, 128 * a - 16:128 * a + 128]) for a in (3, 2, 1)])
-    l_dlt = load([("y", T.dlt[:, 0:16], T.dl[0::2, :]), ("s", T.dlt[:, 16:32], T.dl[1::2, :])])
-    l_val = load([("sy"[w % 2], T.vw[w::16, 0:512], T.val[:, :]) for w in range(16)])
+    def act(out, in_, func, bias=0.0, scale=1.0, deps=()):
+        return do("s", lambda e: e.activation(out, in_, func, bias=bias, scale=scale), deps)
+
+    blk = [(a - r) % 4 for a in range(4)]
+    later = [d for d in range(r + 1, N)]
+
+    parts = []
+    for a in range(4):
+        for q, row in (("y", 8 * blk[a]), ("s", 32 + 8 * blk[a])):
+            lo = max(0, 128 * a - 16)
+            parts.append((q, T.rlc[row:row + 8, :], T.rl[:, lo:lo + 144]))
+    l_rlc = load(parts)
+    l_lst = load([("y", T.lt0[:, 0:16], T.rl[0::2, :]), ("s", T.lt0[:, 16:32], T.rl[1::2, :]),
+                  ("y", T.lt0[:, 32:48], T.dl[0::2, :]), ("s", T.lt0[:, 48:64], T.dl[1::2, :])])
 
     pi = do("g", lambda e: e.iota(T.pi[:, :], [[0, 1]], 0, 1))
     mg = do("g", lambda e: e.iota(T.mg[:, :], [[1, 8], [0, 16]], 0, 0, allow_small_or_imprecise_dtypes=True))
-    hz = do("v", lambda e: e.memset(T.rlc[0:8, 0:16], 0))
-    tz = do("v", lambda e: e.memset(T.sm[:, 32:48], 0.0))
-    kg = ts(T.kg[:, :], T.pi[:, :], 4, A.arith_shift_right, deps=[pi])
+    mi = do("g", lambda e: e.iota(T.mi[:, :], [[1, 128]], 0, 0, allow_small_or_imprecise_dtypes=True))
+    cc = [do("v", lambda e: e.memset(T.ccol[32 * i:32 * i + 32, :], 8.0 + i)) for i in range(2)]
+    fz = do("v", lambda e: e.memset(T.ff[:, 33:65], 0.0))
+    f1 = do("v", lambda e: e.memset(T.ff[:, 32:33], 1.0))
+    tz = do("v", lambda e: e.memset(T.ca[64:128, 128:144], 0.0)) if later else None
+    vn = [do("v", lambda e: e.memset(T.vw[:, 0:4], -2)), do("v", lambda e: e.memset(T.vw[:, 4:16], -1))]
+    pif = do("v", lambda e: e.tensor_copy(T.pif[:, :], T.pi[:, :]), [pi])
+    kg = ts(T.kg[:, :], T.pi[:, :], 4, A.arith_shift_right)
     pa = ts(T.pa[:, :], T.pi[:, :], 15, A.bitwise_and)
     kgf = do("v", lambda e: e.tensor_copy(T.kgf[:, :], T.kg[:, :]), [kg])
+    paf = do("v", lambda e: e.tensor_copy(T.paf[:, :], T.pa[:, :]), [pa])
     sg = ts(T.sg[:, :], T.mg[:, :], T.kgf[:, :], A.is_equal, deps=[mg, kgf])
     lt = do("g", lambda e: e.affine_select(T.lt[:, :], T.sg[:, :], [[-1, 128]], A.is_ge, 0.0, -1, 1), [sg])
-    d2 = do("g", lambda e: e.affine_select(T.d2[:, :], T.sg[:, :], [[1, 128]], A.is_equal, 0.0, -15, -1), [sg])
-    d1 = do("g", lambda e: e.affine_select(T.d1[:, :], T.lt[:, :], [[-1, 128]], A.is_equal, 0.0, -1, 1), [lt])
-    pif = do("v", lambda e: e.tensor_copy(T.pif[:, :], T.pi[:, :]))
-    wcol = ts(T.wcol[:, :], T.pa[:, :], 1.0, A.mult, deps=[pa])
-    mb = ts(T.mb[:, :], T.pa[:, :], -2048.0, A.mult)
-    pcol = ts(T.pcol[:, :], T.pa[:, :], 512.0, A.mult, 480.0, A.add)
-    kcol = ts(T.kcol[:, :], T.pa[:, :], -512.0, A.mult)
-    sel = [ts(T["sel%d" % a][0:32, :], T.mg[0:32, :], 8.0 * a, A.add, T.pif[0:32, :], A.is_equal, [pif]) for a in range(4)]
-    f1 = do("v", lambda e: e.memset(T.f0[:, 32:48], 1.0))
-    vn = do("v", lambda e: e.memset(T.vw[:, 512:528], -1))
-    vz = do("v", lambda e: e.memset(T.vw[:, 528:536], -2))
+    km = [act(T.kmod[32 * i:32 * i + 32, :], T.pif[32 * i:32 * i + 32, :], F.Copy, bias=-32.0 * i, deps=[pif]) for i in range(2)]
+    l_val = load([("sy"[w > 5], T.vw[w::16, 16:528], T.val[:, :]) for w in range(16)])
+    zc = ts(T.zc[:, :], T.paf[:, :], 0.0, A.is_equal, -16.0 * COLS, A.mult, [paf])
+    sel = [ts(T["sel%d" % a][0:64, :], T.mg[0:64, :], 8.0 * blk[a], A.add, T.kmod[0:64, :], A.is_equal, km) for a in range(4)]
 
-    def scaled(out, in_, c, dep):
-        return do("s", lambda e: e.activation(out[:, :], in_[:, :], F.Copy, scale=c), [dep])
-    a1 = scaled(T.a1, T.sg, 0.0625, sg)
-    a3 = scaled(T.a3, T.sg, 32.0, sg)
-    lv = scaled(T.lv, T.lt, -1.0, lt)
-    a2 = scaled(T.a2, T.lt, -0.0625, lt)
-    a4 = scaled(T.a4, T.lt, -32.0, lt)
-    d2s = scaled(T.d2s, T.d2, -8192.0, d2)
+    mb = act(T.mb[:, :], T.paf[:, :], F.Copy, scale=-2048.0, deps=[paf])
+    kcol = act(T.kcol[:, :], T.paf[:, :], F.Copy, scale=-float(COLS))
+    pm1 = act(T.pm1[:, :], T.pif[:, :], F.Copy, bias=-1.0)
+    p15 = act(T.p15[:, :], T.pif[:, :], F.Copy, bias=15.0)
+    sgv = act(T.sgv[:, :], T.sg[:, :], F.Copy, scale=1.0 / 1024, deps=[sg])
+    lvv = act(T.lvv[:, :], T.lt[:, :], F.Copy, scale=-1.0 / 1024, deps=[lt])
 
-    rlw = do("v", lambda e: e.transpose(T.rlw[:, :], T.rlt[:, :]), [l_rlt])
-    if r < N - 1:
-        tail = ts(T.sm[0:8, 32:48], T.tli[0:8, :], 16.0, A.mult, deps=[tz, l_tli])
-    f0 = ts(T.f0[:, 0:32], T.rlw[:, :], 0.0, A.is_equal, deps=[rlw])
-    s0 = scan(T.sm[:, 0:32], T.f0[:, 0:32], T.f0[:, 0:32], 0.0, A.add, A.max, [f0])
-    later = [d for d in range(r + 1, N)]
+    ca = ts(T.ca[0:64, :], T.rlc[0:64, :], -4.0, A.mult, T.ccol[0:64, :], A.add, [l_rlc] + cc)
+    lw = do("v", lambda e: e.transpose(T.lw[:, :], T.lt0[:, :]), [l_lst])
+    cb = ts(T.cb[0:64, :], T.ca[0:64, :], 4.5, A.is_le, 16.0, A.mult, [ca])
+    f0 = ts(T.ff[:, 0:32], T.lw[:, 0:32], 0.0, A.is_equal, deps=[lw])
+    cp = scan(T.cp[0:64, :], T.ca[0:64, :], T.cb[0:64, :], 0.0, A.add, A.min, [cb])
+    sm = scan(T.sm[:, :], T.ff[:, :], T.ff[:, :], 0.0, A.add, A.max, [f0, f1, fz])
+    f2 = ts(T.f2[:, :], T.lw[:, 32:64], 2.0, A.is_equal)
+    s2 = scan(T.s2[:, :], T.f2[:, :], T.f2[:, :], 64.5, A.add, A.max, [f2])
+    idn = ts(T.idn[:, :], T.mi[:, :], T.pif[:, :], A.is_equal, deps=[mi])
+    idh = ts(T.idh[:, :], T.mi[:, :], T.pif[:, :], A.is_equal, -float(COLS), A.mult)
+    d1s = ts(T.d1s[:, :], T.mi[:, :], T.pm1[:, :], A.is_equal, T.kcol[:, :], A.mult, [pm1, kcol])
+    d2s = ts(T.d2s[:, :], T.mi[:, :], T.p15[:, :], A.is_equal, T.zc[:, :], A.mult, [p15, zc])
+
+    n_loc0 = n_loc1 = 0
     if later:
-        after("g", [tail, s0])
-        ids, dsts = [], []
+        rid, pnc = topo.addr(T.cores[r + 1], core)
+        after("g", [ca, tz])
+        g.remote_dma(T.ha[:, 0:16], T.ca[:, 128:144], T.sem["t"], T.sem["loc0"], pnc, rid, topo.mask(core, T.cores[r + 1]))
+        n_loc0 = len(topo.engines(core, T.cores[r + 1]))
+        after("g", [sm])
+        ids = []
         for d in reversed(later):
             rid, pnc = topo.addr(T.cores[d], core)
             ids.append(DstId(rid=rid, pnc=pnc))
-            dsts.append(T.rbh[:, 15:32] if d == r + 1 else T["msg%d" % r][:, 0:17])
         g.remote_dma_fused([RemoteDMATransfer(dst_ids=ids, dma_engine_mask=topo.mask(core, T.cores[later[0]]),
-                                              remote_sem=T.sem["m%d" % r], srcs=[T.sm[:, 31:48]], dsts=dsts)],
-                           local_sem=T.sem["loc1"])
+                                              remote_sem=T.sem["m%d" % r], srcs=[T.sm[:, 33:65]],
+                                              dsts=[T["msg%d" % r][:, :] for d in later])], local_sem=T.sem["loc1"])
         n_loc1 = len(topo.engines(core, T.cores[later[0]]))
+    wf = do("g", lambda e: e.iota(T.win[:, 0:COLS], [[0, COLS]], -2, 0, allow_small_or_imprecise_dtypes=True))
 
-    rb = ts(T.rb[0:32, :], T.rlc[0:32, :], 16.0, A.mult, deps=[hz, l_rlc])
-    d0 = do("s", lambda e: e.activation(T.d0[0:32, :], T.rb[0:32, :], F.Copy, bias=-31.0), [rb])
-    rst = do("s", lambda e: e.activation(T.rst[0:32, :], T.rb[0:32, 16:144], F.Copy, bias=-2.0, scale=float(1 << 17)))
-    one4 = ts(T.one4[0:32, :], T.rb[0:32, :], 16.0, A.is_equal, 4.0, A.mult, [rb])
-    dlw = do("v", lambda e: e.transpose(T.dlw[:, :], T.dlt[:, :]), [l_dlt])
-    ls = scan(T.ls[0:32, :], T.one4[0:32, :], T.rb[0:32, :], 0.0, A.add, A.min, [one4])
-    f2 = ts(T.f2[:, :], T.dlw[:, :], 2.0, A.is_equal, deps=[dlw])
-    cap = ts(T.cap[:, :], T.dlw[:, :], -520.0, A.mult, 1041.0, A.add)
-    pl = scan(T.pl[0:32, :], T.d0[0:32, :], T.ls[0:32, :], 0.0, A.add, A.max, [d0, ls])
-    s2 = scan(T.s2[:, :], T.f2[:, :], T.f2[:, :], 0.0, A.add, A.max, [f2])
-    d1s = ts(T.d1s[:, :], T.d1[:, :], T.kcol[:, :], A.mult, deps=[kcol, d1])
-    wf = do("v", lambda e: e.memset(T.win[:, 0:512], -2.0))
-
-    psw = []
-    for a in range(4):
-        psw.append(mat(T["psw%d" % (a // 2)][:, 128 * (a % 2):128 * (a % 2) + 128], T["sel%d" % a][0:32, :], T.pl[0:32, 16:144],
-                       True, True, [sel[a], pl]))
-        if a == 1:
-            v1 = mat(T.psv[:, 0:32], T.lv[:, :], T.f2[:, :], True, False, [lv, f2])
-            v2 = mat(T.psv[:, 0:32], T.sg[:, :], T.s2[:, :], False, True, [sg, s2])
-    psr = [mat(T.psr[:, 128 * a:128 * a + 128], T["sel%d" % a][0:32, :], T.rst[0:32, :], True, True, [rst]) for a in range(4)]
-    ps1 = [mat(T.ps1[:, 0:32], T.a1[:, :], T.sm[:, 0:32], True, False, [a1, s0]),
-           mat(T.ps1[:, 0:32], T.a2[:, :], T.f0[:, 0:32], False, True, [a2, f0])]
-    ps2 = [mat(T.ps2[:, 0:32], T.a3[:, :], T.sm[:, 0:32], True, False, [a3]),
-           mat(T.ps2[:, 0:32], T.a4[:, :], T.f0[:, 0:32], False, False, [a4]),
-           mat(T.ps2[:, 0:32], T.d1s[:, :], T.f0[:, 0:32], False, False, [d1s]),
-           mat(T.ps2[:, 0:32], T.d2s[:, :], T.f0[:, 1:33], False, True, [d2s, f1])]
-
-    ovf = do("v", lambda e: e.tensor_tensor(T.ovf[:, :], T.cap[:, :], T.psv[:, 0:32], A.max), [cap, v1, v2])
-    offv = ts(T.offv[:, :], T.ovf[:, :], -1.0, A.add, 528.0, A.min, [ovf])
-    mask = [do("s", lambda e: e.activation(T.mask[:, 256 * h:256 * h + 256], T["psw%d" % h][:, 0:256], F.Square,
-                                           bias=T.mb[:, :], scale=2048.0), [psw[2 * h], psw[2 * h + 1], mb]) for h in range(2)]
-    mm = [do("v", lambda e: e.tensor_tensor(T.mm[:, 256 * h:256 * h + 256], T.vw[:, 0:VWW].indirect(T.offv[:, 16 * h:16 * h + 16]),
-                                            T.mask[:, 256 * h:256 * h + 256], A.subtract), [l_val, vn, vz, offv, mask[h]])
-          for h in range(2)]
-    vv = scan(T.vv[:, :], T.psr[:, :], T.mm[:, :], -2.0, A.min, A.max, psr + mm)
-
+    rst = act(T.rst[0:32, :], T.cb[0:32, :], F.Copy, bias=-2.0, scale=float(1 << 17), deps=[cb])
     if r:
-        own = ts(T.rbh[0:8, 32:48], T.rlc[0:8, 16:32], 16.0, A.mult)
-        heads = [("m%d" % p, len(topo.engines(T.cores[p], core))) for p in range(r)]
-        cnt = [T["msg%d" % p][:, 0:1] for p in range(r - 1)] + [T.rbh[:, 15:16]]
-        one4h = ts(T.one4h[0:8, :], T.rbh[0:8, 16:48], 16.0, A.is_equal, 4.0, A.mult, [own, heads[-1]])
-        d0h = ts(T.d0h[0:8, :], T.rbh[0:8, 16:48], -31.0, A.add)
-        lsh = scan(T.lsh[0:8, :], T.one4h[0:8, :], T.rbh[0:8, 16:48], 0.0, A.add, A.min, [one4h])
-        plh = scan(T.plh[0:8, :], T.d0h[0:8, :], T.lsh[0:8, :], 0.0, A.add, A.max, [d0h, lsh])
-        base = []
-        for col, m in ((0, T.a1), (1, T.a3)):
-            for p in range(r):
-                base.append(mat(T.psb[:, col:col + 1], m[:, :], cnt[p], p == 0, p == r - 1, [heads[p]]))
-        psh = mat(T.psh[:, 0:16], T.sel0[0:8, :], T.plh[0:8, 16:32], True, True, [plh])
-        hi = ts(T.hi[:, :], T.ps1[:, 0:32], T.psb[:, 0:1], A.add, -17.0 / 32, A.add, ps1 + base)
-        uu = ts(T.uu[:, :], T.hi[:, :], -511.0, A.mult, T.pcol[:, :], A.add, [hi, pcol])
-        maskh = ts(T.maskh[:, :], T.psh[:, 0:16], T.wcol[:, :], A.not_equal, BIG, A.mult, [psh, wcol])
-        zz = do("v", lambda e: e.tensor_tensor(T.zz[:, :], T.uu[:, :], T.ps2[:, 0:32], A.add), [uu] + ps2)
-        mmh = do("v", lambda e: e.tensor_tensor(T.mmh[:, :], T.vw[:, 0:VWW].indirect(T.offv[:, 0:1]), T.maskh[:, :], A.subtract),
-                 [maskh])
-        offs = ts(T.offs[:, :], T.zz[:, :], T.psb[:, 1:2], A.add, deps=[zz])
-        done = scan(T.vv[:, 0:16], T.psr[:, 0:16], T.mmh[:, :], -2.0, A.min, A.max, [mmh, vv])
-    else:
-        hi = ts(T.hi[:, :], T.ps1[:, 0:32], -17.0 / 32, A.add, deps=ps1)
-        uu = ts(T.uu[:, :], T.hi[:, :], -511.0, A.mult, T.pcol[:, :], A.add, [hi, pcol])
-        zz = do("v", lambda e: e.tensor_tensor(T.zz[:, :], T.uu[:, :], T.ps2[:, 0:32], A.add), [uu] + ps2)
-        offs = do("v", lambda e: e.tensor_copy(T.offs[:, :], T.zz[:, :]), [zz])
-        done = vv
+        hac = act(T.ha[0:64, 16:48], T.ca[0:64, 0:32], F.Copy, deps=[ca])
+    psw = {}
+    for a in (2, 3, 0, 1):
+        lo = 16 if a else 0
+        psw[a] = mat(T["psw%d" % (a // 2)][:, 128 * (a % 2):128 * (a % 2) + 128], T["sel%d" % a][0:64, :], T.cp[0:64, lo:lo + 128],
+                     True, True, [sel[a], cp])
+        if a == 3:
+            v1 = mat(T.psv[:, 0:32], T.lvv[:, :], T.f2[:, :], True, False, [lvv, f2])
+            v2 = mat(T.psv[:, 0:32], T.sgv[:, :], T.s2[:, :], False, True, [sgv, s2])
+    psr = []
+    for a in range(4):
+        lo = 16 if a else 0
+        psr.append(mat(T.psr[:, 128 * a:128 * a + 128], T["sel%d" % a][0:32, :], T.rst[0:32, lo:lo + 128], True, True, [rst]))
+    mask = {}
 
-    sc = do("v", lambda e: e.tensor_copy(T.win[:, 0:WINW].indirect(T.offs[:, 0:32]), T.vv[:, :]), [offs, done, wf])
+    def masks(h):
+        mask[h] = act(T.mask[:, 256 * h:256 * h + 256], T["psw%d" % h][:, 0:256], F.Square, bias=T.mb[:, :], scale=2048.0,
+                      deps=[psw[2 * h], psw[2 * h + 1], mb])
+    masks(1)
+    sgr = act(T.sgr[:, :], T.sg[:, :], F.Copy, scale=float(H))
+    ltr = act(T.ltr[:, :], T.lt[:, :], F.Copy, scale=-float(H))
+    masks(0)
+    pcol = act(T.pcol[:, :], T.paf[:, :], F.Copy, scale=float(COLS),
+               bias=float(COLS - H - 16 * r * H + 129 * (COLS - 1) - 2 * r))
+
+    mn = tt(T.mn[:, :], T.lw[:, 32:64], T.psv[:, 0:32], A.min, [v1, v2])
+    offv = ts(T.offv[:, :], T.mn[:, :], 1024.0, A.mult, -1017.0, A.add, [mn])
+
+    def gather(lo, hi, in1, deps):
+        return tt(T.mm[:, lo:hi], T.vw[:, :].indirect(T.offv[:, lo // 16:hi // 16]), in1, A.subtract, deps)
+    mm = [gather(256, 512, T.mask[:, 256:512], [l_val, offv, mask[1]] + vn)]
+    heads = [("m%d" % p, len(topo.engines(T.cores[p], core))) for p in range(r)]
+    p1 = [mat(T.ps1[:, 0:32], T.sgr[:, :], T.sm[:, 0:32], True, False, [sgr, sm]),
+          mat(T.ps1[:, 0:32], T.ltr[:, :], T.ff[:, 0:32], False, not r, [ltr, f0])]
+    p2 = [mat(T.ps2[:, 0:32], T.sgr[:, :], T.sm[:, 0:32], True, False),
+          mat(T.ps2[:, 0:32], T.ltr[:, :], T.ff[:, 0:32], False, False),
+          mat(T.ps2[:, 0:32], T.d1s[:, :], T.ff[:, 0:32], False, False, [d1s]),
+          mat(T.ps2[:, 0:32], T.d2s[:, :], T.ff[:, 1:33], False, False, [d2s, f1])]
+    if r:
+        hb = ts(T.hb[0:64, :], T.ha[0:64, :], 4.5, A.is_le, 16.0, A.mult, [hac, ("t", len(topo.engines(T.cores[r - 1], core)))])
+        hp = scan(T.hp[0:64, :], T.ha[0:64, :], T.hb[0:64, :], 0.0, A.add, A.min, [hb])
+        psh = mat(T.psh[:, 0:32], T.sel0[0:64, :], T.hp[0:64, 16:48], True, True, [hp])
+        maskh = act(T.maskh[:, :], T.psh[:, 0:32], F.Square, bias=T.mb[:, :], scale=2048.0, deps=[psh])
+        for p in range(r):
+            p1.append(mat(T.ps1[:, 0:32], T.sgr[:, :], T["msg%d" % p][:, :], False, p == r - 1, [heads[p]]))
+        for p in range(r):
+            p2.append(mat(T.ps2[:, 0:32], T.sgr[:, :], T["msg%d" % p][:, :], False, False))
+    mm.append(gather(32 if r else 0, 256, T.mask[:, 32 if r else 0:256], [mask[0]]))
+    if r:
+        mm.append(gather(0, 32, T.maskh[:, :], [maskh]))
+    hh = ts(T.hh[:, :], T.ps1[:, 0:32], 1.0 / COLS, A.mult, 129.0 - 17.0 / 32 - r, A.add, p1)
+    p2.append(mat(T.ps2[:, 0:32], T.idn[:, :], T.hh[:, :], False, False, [hh, idn]))
+    p2.append(mat(T.ps2[:, 0:32], T.idh[:, :], T.hh[:, :], False, True, [idh]))
+    vv = scan(T.vv[:, :], T.psr[:, :], T.mm[:, :], -2.0, A.min, A.max, psr + mm)
+    offs = ts(T.offs[:, :], T.ps2[:, 0:32], T.pcol[:, :], A.add, deps=p2 + [pcol])
+
+    sc = do("v", lambda e: e.tensor_copy(T.win[:, :].indirect(T.offs[:, :]), T.vv[:, :]), [offs, vv, wf])
 
     after("g", [sc])
     n_loc2 = 0
     for k in range(1, N):
         d = (r + k) % N
         rid, pnc = topo.addr(T.cores[d], core)
-        g.remote_dma(T["from%d" % r][:, :], T.win[:, 128 * d:128 * d + 128], T.sem["h%d" % r], T.sem["loc2"],
+        g.remote_dma(T["from%d" % r][:, :, :], T.win[:, BLK * d:BLK * d + BLK], T.sem["h%d" % r], T.sem["loc2"],
                      pnc, rid, topo.mask(core, T.cores[d]))
         n_loc2 += len(topo.engines(core, T.cores[d]))
-    src = [p for p in range(N) if p != r]
-    arr = [("h%d" % p, len(topo.engines(T.cores[p], core))) for p in src]
-    land = [T["from%d" % p] for p in src]
-    c1 = do("v", lambda e: e.tensor_tensor(T.acc1[:, :], T.win[:, 128 * r:128 * r + 128], land[0][:, :], A.max), [sc, arr[0]])
-    c2 = do("v", lambda e: e.tensor_tensor(T.acc2[:, :], T.acc1[:, :], land[1][:, :], A.max), [c1, arr[1]])
-    ta = [do("v", lambda e: e.transpose(T.ta[:, b, :], T.acc2[:, 32 * b:32 * b + 32]), [c2]) for b in range(4)]
-    tl = [do("v", lambda e: e.transpose(T.tl[:, b, :], land[2][:, 32 * b:32 * b + 32]), [arr[2]]) for b in range(4)]
-    fin = [do("v", lambda e: e.tensor_tensor(T.fin[:, h, :, :], T.ta[:, :, 16 * h:16 * h + 16], T.tl[:, :, 16 * h:16 * h + 16], A.max),
-              ta + tl) for h in range(2)]
+    az = do("v", lambda e: e.memset(T.acc[:, :, :], -2.0))
+    m = [do("v", lambda e: e.tensor_copy(T.acc[:, b, 2 * r:2 * r + H], T.win[:, BLK * r + H * b:BLK * r + H * b + H]), [az, sc])
+         for b in range(4)]
+    for k in range(1, N):
+        p = (r - k) % N
+        part = T.acc[:, :, 2 * p:2 * p + H]
+        m = [tt(part, part, T["from%d" % p][:, :, :], A.max, m + [("h%d" % p, len(topo.engines(T.cores[p], core)))])]
+    ta = [do("v", lambda e: e.transpose(T.ta[:, b, :], T.acc[:, b, :]), m) for b in range(4)]
+    fin = [do("v", lambda e: e.tensor_copy(T.fin[:, 0, :, :], T.ta[:, :, 0:16]), ta),
+           act(T.fin[:, 1, :, :], T.ta[:, :, 16:32], F.Copy, deps=ta)]
     for h, q in enumerate("ys"):
         after(q, [fin[h]])
         n = new()
         queues[q].dma_start(T.y[h::2, :], T.fin[:, h, :, :]).then_inc(T.sem[n], 16)
         after(q, [(n, 16)])
 
-    if later:
-        g.wait_ge(T.sem["loc1"], n_loc1)
-    g.wait_ge(T.sem["loc2"], n_loc2)
+    for n, c in (("loc0", n_loc0), ("loc1", n_loc1), ("loc2", n_loc2)):
+        if c:
+            g.wait_ge(T.sem[n], c)
     waited = [d[0] for q in seen for d in seen[q]]
     for n in used:
         if n not in waited:

from concourse.bass import DstId, RemoteDMATransfer
from concourse.mybir import AluOpType as A, ActivationFunctionType as F

H = 26
BLK, COLS = 4 * H, 16 * H
WINW = 17 * COLS
VWW = 16 + 512
I32, F32, B16, U16 = "int32", "float32", "bfloat16", "uint16"


def sb(width, dtype):
    return ("sbuf", [128] + (width if isinstance(width, list) else [width]), dtype)


SCRATCH = {
    "lt0": sb(64, I32), "lw": sb(64, I32), "rlc": sb(144, I32), "vw": sb(VWW, I32),
    "ff": sb(65, B16), "sm": sb(65, B16), "f2": sb(32, B16), "s2": sb(32, B16),
    "mn": sb(32, F32), "offv": sb(32, U16), "offs": sb(32, U16), "hh": sb(32, B16),
    "ca": sb(144, B16), "cb": sb(144, B16), "cp": sb(144, B16), "rst": sb(144, B16),
    "ha": sb(48, B16), "hb": sb(48, B16), "hp": sb(48, B16),
    "mask": sb(512, B16), "maskh": sb(32, B16), "mm": sb(512, F32), "vv": sb(512, F32), "win": sb(WINW, F32),
    "msg0": sb(32, B16), "msg1": sb(32, B16), "msg2": sb(32, B16),
    "from0": sb([4, H], F32), "from1": sb([4, H], F32), "from2": sb([4, H], F32), "from3": sb([4, H], F32),
    "acc": sb([4, 32], F32), "ta": sb([4, 32], F32), "fin": sb([2, 4, 16], F32),
    "mg": sb(128, B16), "mi": sb(128, B16), "sg": sb(128, B16), "lt": sb(128, B16), "idn": sb(128, B16), "idh": sb(128, B16),
    "sel0": sb(128, B16), "sel1": sb(128, B16), "sel2": sb(128, B16), "sel3": sb(128, B16),
    "sgv": sb(128, B16), "lvv": sb(128, B16), "sgr": sb(128, B16), "ltr": sb(128, B16),
    "d1s": sb(128, B16), "d2s": sb(128, B16),
    "pi": sb(1, I32), "pa": sb(1, I32), "kg": sb(1, I32), "pif": sb(1, F32), "paf": sb(1, F32), "kgf": sb(1, F32),
    "kmod": sb(1, F32), "pm1": sb(1, F32), "p15": sb(1, F32), "zc": sb(1, F32),
    "ccol": sb(1, F32), "mb": sb(1, F32), "pcol": sb(1, F32), "kcol": sb(1, F32),
}
for _b in ("ps1", "ps2", "psv", "psh", "psw0", "psw1", "psr"):
    SCRATCH[_b] = ("psum", [128, 512], "float32")
SEMAPHORES = ["s%d" % i for i in range(110)] + ["m0", "m1", "m2", "t", "h0", "h1", "h2", "h3", "loc0", "loc1", "loc2"]


def rank_program(g, core, T, topo):
    r = T.rank_of(core)
    if r is None:
        return
    N = len(T.cores)
    queues = {"g": g, "v": g.vector, "s": g.scalar, "p": g.tensor, "y": g.sync}
    seen = {q: [] for q in queues}
    used = []

    def after(q, deps):
        for d in deps:
            if d not in seen[q]:
                queues[q].wait_ge(T.sem[d[0]], d[1])
                seen[q].append(d)

    def new():
        used.append("s%d" % len(used))
        return used[-1]

    def do(q, call, deps=()):
        after(q, deps)
        n = new()
        call(queues[q]).then_inc(T.sem[n], 1)
        return (n, 1)

    def load(parts):
        n = new()
        for q, out, in_ in parts:
            queues[q].dma_start(out, in_).then_inc(T.sem[n], 16)
        return (n, 16 * len(parts))

    def ts(out, in0, s1, op0, s2=None, op1=None, deps=()):
        if op1 is None:
            return do("v", lambda e: e.tensor_scalar(out, in0, s1, None, op0), deps)
        return do("v", lambda e: e.tensor_scalar(out, in0, s1, s2, op0, op1), deps)

    def scan(out, x0, x1, initial, op0, op1, deps=()):
        return do("v", lambda e: e.tensor_tensor_scan(out, x0, x1, initial, op0, op1), deps)

    def tt(out, in0, in1, op, deps=()):
        return do("v", lambda e: e.tensor_tensor(out, in0, in1, op), deps)

    def mat(out, lhs, rhs, start, stop, deps=()):
        return do("p", lambda e: e.matmul(out, lhs, rhs, start, stop), deps)

    def act(out, in_, func, bias=0.0, scale=1.0, deps=()):
        return do("s", lambda e: e.activation(out, in_, func, bias=bias, scale=scale), deps)

    blk = [(a - r) % 4 for a in range(4)]
    later = [d for d in range(r + 1, N)]

    parts = []
    for a in range(4):
        for q, row in (("y", 8 * blk[a]), ("s", 32 + 8 * blk[a])):
            lo = max(0, 128 * a - 16)
            parts.append((q, T.rlc[row:row + 8, :], T.rl[:, lo:lo + 144]))
    l_rlc = load(parts)
    l_lst = load([("y", T.lt0[:, 0:16], T.rl[0::2, :]), ("s", T.lt0[:, 16:32], T.rl[1::2, :]),
                  ("y", T.lt0[:, 32:48], T.dl[0::2, :]), ("s", T.lt0[:, 48:64], T.dl[1::2, :])])

    pi = do("g", lambda e: e.iota(T.pi[:, :], [[0, 1]], 0, 1))
    mg = do("g", lambda e: e.iota(T.mg[:, :], [[1, 8], [0, 16]], 0, 0, allow_small_or_imprecise_dtypes=True))
    mi = do("g", lambda e: e.iota(T.mi[:, :], [[1, 128]], 0, 0, allow_small_or_imprecise_dtypes=True))
    cc = [do("v", lambda e: e.memset(T.ccol[32 * i:32 * i + 32, :], 8.0 + i)) for i in range(2)]
    fz = do("v", lambda e: e.memset(T.ff[:, 33:65], 0.0))
    f1 = do("v", lambda e: e.memset(T.ff[:, 32:33], 1.0))
    tz = do("v", lambda e: e.memset(T.ca[64:128, 128:144], 0.0)) if later else None
    vn = [do("v", lambda e: e.memset(T.vw[:, 0:4], -2)), do("v", lambda e: e.memset(T.vw[:, 4:16], -1))]
    pif = do("v", lambda e: e.tensor_copy(T.pif[:, :], T.pi[:, :]), [pi])
    kg = ts(T.kg[:, :], T.pi[:, :], 4, A.arith_shift_right)
    pa = ts(T.pa[:, :], T.pi[:, :], 15, A.bitwise_and)
    kgf = do("v", lambda e: e.tensor_copy(T.kgf[:, :], T.kg[:, :]), [kg])
    paf = do("v", lambda e: e.tensor_copy(T.paf[:, :], T.pa[:, :]), [pa])
    sg = ts(T.sg[:, :], T.mg[:, :], T.kgf[:, :], A.is_equal, deps=[mg, kgf])
    lt = do("g", lambda e: e.affine_select(T.lt[:, :], T.sg[:, :], [[-1, 128]], A.is_ge, 0.0, -1, 1), [sg])
    km = [act(T.kmod[32 * i:32 * i + 32, :], T.pif[32 * i:32 * i + 32, :], F.Copy, bias=-32.0 * i, deps=[pif]) for i in range(2)]
    l_val = load([("sy"[w > 5], T.vw[w::16, 16:528], T.val[:, :]) for w in range(16)])
    zc = ts(T.zc[:, :], T.paf[:, :], 0.0, A.is_equal, -16.0 * COLS, A.mult, [paf])
    sel = [ts(T["sel%d" % a][0:64, :], T.mg[0:64, :], 8.0 * blk[a], A.add, T.kmod[0:64, :], A.is_equal, km) for a in range(4)]

    mb = act(T.mb[:, :], T.paf[:, :], F.Copy, scale=-2048.0, deps=[paf])
    kcol = act(T.kcol[:, :], T.paf[:, :], F.Copy, scale=-float(COLS))
    pm1 = act(T.pm1[:, :], T.pif[:, :], F.Copy, bias=-1.0)
    p15 = act(T.p15[:, :], T.pif[:, :], F.Copy, bias=15.0)
    sgv = act(T.sgv[:, :], T.sg[:, :], F.Copy, scale=1.0 / 1024, deps=[sg])
    lvv = act(T.lvv[:, :], T.lt[:, :], F.Copy, scale=-1.0 / 1024, deps=[lt])

    ca = ts(T.ca[0:64, :], T.rlc[0:64, :], -4.0, A.mult, T.ccol[0:64, :], A.add, [l_rlc] + cc)
    lw = do("v", lambda e: e.transpose(T.lw[:, :], T.lt0[:, :]), [l_lst])
    cb = ts(T.cb[0:64, :], T.ca[0:64, :], 4.5, A.is_le, 16.0, A.mult, [ca])
    f0 = ts(T.ff[:, 0:32], T.lw[:, 0:32], 0.0, A.is_equal, deps=[lw])
    cp = scan(T.cp[0:64, :], T.ca[0:64, :], T.cb[0:64, :], 0.0, A.add, A.min, [cb])
    sm = scan(T.sm[:, :], T.ff[:, :], T.ff[:, :], 0.0, A.add, A.max, [f0, f1, fz])
    f2 = ts(T.f2[:, :], T.lw[:, 32:64], 2.0, A.is_equal)
    s2 = scan(T.s2[:, :], T.f2[:, :], T.f2[:, :], 64.5, A.add, A.max, [f2])
    idn = ts(T.idn[:, :], T.mi[:, :], T.pif[:, :], A.is_equal, deps=[mi])
    idh = ts(T.idh[:, :], T.mi[:, :], T.pif[:, :], A.is_equal, -float(COLS), A.mult)
    d1s = ts(T.d1s[:, :], T.mi[:, :], T.pm1[:, :], A.is_equal, T.kcol[:, :], A.mult, [pm1, kcol])
    d2s = ts(T.d2s[:, :], T.mi[:, :], T.p15[:, :], A.is_equal, T.zc[:, :], A.mult, [p15, zc])

    n_loc0 = n_loc1 = 0
    if later:
        rid, pnc = topo.addr(T.cores[r + 1], core)
        after("g", [ca, tz])
        g.remote_dma(T.ha[:, 0:16], T.ca[:, 128:144], T.sem["t"], T.sem["loc0"], pnc, rid, topo.mask(core, T.cores[r + 1]))
        n_loc0 = len(topo.engines(core, T.cores[r + 1]))
        after("g", [sm])
        ids = []
        for d in reversed(later):
            rid, pnc = topo.addr(T.cores[d], core)
            ids.append(DstId(rid=rid, pnc=pnc))
        g.remote_dma_fused([RemoteDMATransfer(dst_ids=ids, dma_engine_mask=topo.mask(core, T.cores[later[0]]),
                                              remote_sem=T.sem["m%d" % r], srcs=[T.sm[:, 33:65]],
                                              dsts=[T["msg%d" % r][:, :] for d in later])], local_sem=T.sem["loc1"])
        n_loc1 = len(topo.engines(core, T.cores[later[0]]))
    wf = do("g", lambda e: e.iota(T.win[:, 0:COLS], [[0, COLS]], -2, 0, allow_small_or_imprecise_dtypes=True))

    rst = act(T.rst[0:32, :], T.cb[0:32, :], F.Copy, bias=-2.0, scale=float(1 << 17), deps=[cb])
    if r:
        hac = act(T.ha[0:64, 16:48], T.ca[0:64, 0:32], F.Copy, deps=[ca])
    psw = {}
    for a in (2, 3, 0, 1):
        lo = 16 if a else 0
        psw[a] = mat(T["psw%d" % (a // 2)][:, 128 * (a % 2):128 * (a % 2) + 128], T["sel%d" % a][0:64, :], T.cp[0:64, lo:lo + 128],
                     True, True, [sel[a], cp])
        if a == 3:
            v1 = mat(T.psv[:, 0:32], T.lvv[:, :], T.f2[:, :], True, False, [lvv, f2])
            v2 = mat(T.psv[:, 0:32], T.sgv[:, :], T.s2[:, :], False, True, [sgv, s2])
    psr = []
    for a in range(4):
        lo = 16 if a else 0
        psr.append(mat(T.psr[:, 128 * a:128 * a + 128], T["sel%d" % a][0:32, :], T.rst[0:32, lo:lo + 128], True, True, [rst]))
    mask = {}

    def masks(h):
        mask[h] = act(T.mask[:, 256 * h:256 * h + 256], T["psw%d" % h][:, 0:256], F.Square, bias=T.mb[:, :], scale=2048.0,
                      deps=[psw[2 * h], psw[2 * h + 1], mb])
    masks(1)
    sgr = act(T.sgr[:, :], T.sg[:, :], F.Copy, scale=float(H))
    ltr = act(T.ltr[:, :], T.lt[:, :], F.Copy, scale=-float(H))
    masks(0)
    pcol = act(T.pcol[:, :], T.paf[:, :], F.Copy, scale=float(COLS),
               bias=float(COLS - H - 16 * r * H + 129 * (COLS - 1) - 2 * r))

    mn = tt(T.mn[:, :], T.lw[:, 32:64], T.psv[:, 0:32], A.min, [v1, v2])
    offv = ts(T.offv[:, :], T.mn[:, :], 1024.0, A.mult, -1017.0, A.add, [mn])

    def gather(lo, hi, in1, deps):
        return tt(T.mm[:, lo:hi], T.vw[:, :].indirect(T.offv[:, lo // 16:hi // 16]), in1, A.subtract, deps)
    mm = [gather(256, 512, T.mask[:, 256:512], [l_val, offv, mask[1]] + vn)]
    heads = [("m%d" % p, len(topo.engines(T.cores[p], core))) for p in range(r)]
    p1 = [mat(T.ps1[:, 0:32], T.sgr[:, :], T.sm[:, 0:32], True, False, [sgr, sm]),
          mat(T.ps1[:, 0:32], T.ltr[:, :], T.ff[:, 0:32], False, not r, [ltr, f0])]
    p2 = [mat(T.ps2[:, 0:32], T.sgr[:, :], T.sm[:, 0:32], True, False),
          mat(T.ps2[:, 0:32], T.ltr[:, :], T.ff[:, 0:32], False, False),
          mat(T.ps2[:, 0:32], T.d1s[:, :], T.ff[:, 0:32], False, False, [d1s]),
          mat(T.ps2[:, 0:32], T.d2s[:, :], T.ff[:, 1:33], False, False, [d2s, f1])]
    if r:
        hb = ts(T.hb[0:64, :], T.ha[0:64, :], 4.5, A.is_le, 16.0, A.mult, [hac, ("t", len(topo.engines(T.cores[r - 1], core)))])
        hp = scan(T.hp[0:64, :], T.ha[0:64, :], T.hb[0:64, :], 0.0, A.add, A.min, [hb])
        psh = mat(T.psh[:, 0:32], T.sel0[0:64, :], T.hp[0:64, 16:48], True, True, [hp])
        maskh = act(T.maskh[:, :], T.psh[:, 0:32], F.Square, bias=T.mb[:, :], scale=2048.0, deps=[psh])
        for p in range(r):
            p1.append(mat(T.ps1[:, 0:32], T.sgr[:, :], T["msg%d" % p][:, :], False, p == r - 1, [heads[p]]))
        for p in range(r):
            p2.append(mat(T.ps2[:, 0:32], T.sgr[:, :], T["msg%d" % p][:, :], False, False))
    mm.append(gather(32 if r else 0, 256, T.mask[:, 32 if r else 0:256], [mask[0]]))
    if r:
        mm.append(gather(0, 32, T.maskh[:, :], [maskh]))
    hh = ts(T.hh[:, :], T.ps1[:, 0:32], 1.0 / COLS, A.mult, 129.0 - 17.0 / 32 - r, A.add, p1)
    p2.append(mat(T.ps2[:, 0:32], T.idn[:, :], T.hh[:, :], False, False, [hh, idn]))
    p2.append(mat(T.ps2[:, 0:32], T.idh[:, :], T.hh[:, :], False, True, [idh]))
    vv = scan(T.vv[:, :], T.psr[:, :], T.mm[:, :], -2.0, A.min, A.max, psr + mm)
    offs = ts(T.offs[:, :], T.ps2[:, 0:32], T.pcol[:, :], A.add, deps=p2 + [pcol])

    sc = do("v", lambda e: e.tensor_copy(T.win[:, :].indirect(T.offs[:, :]), T.vv[:, :]), [offs, vv, wf])

    after("g", [sc])
    n_loc2 = 0
    for k in range(1, N):
        d = (r + k) % N
        rid, pnc = topo.addr(T.cores[d], core)
        g.remote_dma(T["from%d" % r][:, :, :], T.win[:, BLK * d:BLK * d + BLK], T.sem["h%d" % r], T.sem["loc2"],
                     pnc, rid, topo.mask(core, T.cores[d]))
        n_loc2 += len(topo.engines(core, T.cores[d]))
    az = do("v", lambda e: e.memset(T.acc[:, :, :], -2.0))
    m = [do("v", lambda e: e.tensor_copy(T.acc[:, b, 2 * r:2 * r + H], T.win[:, BLK * r + H * b:BLK * r + H * b + H]), [az, sc])
         for b in range(4)]
    for k in range(1, N):
        p = (r - k) % N
        part = T.acc[:, :, 2 * p:2 * p + H]
        m = [tt(part, part, T["from%d" % p][:, :, :], A.max, m + [("h%d" % p, len(topo.engines(T.cores[p], core)))])]
    ta = [do("v", lambda e: e.transpose(T.ta[:, b, :], T.acc[:, b, :]), m) for b in range(4)]
    fin = [do("v", lambda e: e.tensor_copy(T.fin[:, 0, :, :], T.ta[:, :, 0:16]), ta),
           act(T.fin[:, 1, :, :], T.ta[:, :, 16:32], F.Copy, deps=ta)]
    for h, q in enumerate("ys"):
        after(q, [fin[h]])
        n = new()
        queues[q].dma_start(T.y[h::2, :], T.fin[:, h, :, :]).then_inc(T.sem[n], 16)
        after(q, [(n, 16)])

    for n, c in (("loc0", n_loc0), ("loc1", n_loc1), ("loc2", n_loc2)):
        if c:
            g.wait_ge(T.sem[n], c)
    waited = [d[0] for q in seen for d in seen[q]]
    for n in used:
        if n not in waited:
            g.wait_ge(T.sem[n], 1)
